import numpy as np, ml_dtypes
CORES = [35,38,43,46]
N = 4
import mx_ref
BF = ml_dtypes.bfloat16
def pick(q, e):
    c = np.concatenate([q[0].reshape(128, -1, 4), np.zeros((128, 1, 4), np.uint8)], axis=1); s = np.concatenate([q[1], np.ones((16, 1), np.uint8)], axis=1)
    return (np.ascontiguousarray(c[:, e].reshape(128, -1)), np.ascontiguousarray(s[:, e]))
def join(*qs):
    return (np.concatenate([q[0] for q in qs], axis=1), np.concatenate([q[1] for q in qs], axis=1))
def put(q, e, v):
    c, s = q[0].reshape(128, -1, 4).copy(), q[1].copy(); c[:, e] = v[0].reshape(128, -1, 4); s[:, e] = v[1]
    return (c.reshape(128, -1), s)
def pk(c, s):
    return (np.ascontiguousarray(c), mx_ref.live(s))
def emit(q):
    return q[0], q[1]
def cols(t, e):
    v = np.concatenate([t.reshape(128, -1, 4), np.zeros((128, 1, 4), BF)], axis=1)
    return np.ascontiguousarray(v[:, e]).reshape(128, -1)
def tile(rs):
    return np.stack(rs, axis=2).reshape(128, -1).astype(BF)
def decode(q):
    o = []
    for b in range(4):
        e = np.zeros((128, 128, 4), np.float32); e[np.arange(128), np.arange(128), b] = 1
        o.append(mx_ref.matmul(mx_ref.quantize(e.reshape(128, 512).astype(BF)), q))
    return np.stack(o, axis=2).reshape(128, -1)
def f(rng, *shape):
    return mx_ref.flush((rng.standard_normal(shape, dtype=np.float32) * np.exp2(rng.integers(-2, 3, shape[:-1] + (1,)))).astype(BF))
def wide(rng, *shape, cols=0):
    v = rng.standard_normal(shape, dtype=np.float32) * np.exp2(rng.integers(-12, 13, shape)).astype(np.float32)
    if cols: v *= np.repeat(np.exp2(rng.integers(-cols, cols + 1, shape[:-2] + (1, shape[-1] // 4))) * (rng.random(shape[:-2] + (1, shape[-1] // 4)) > 0.0625), 4, axis=-1).astype(np.float32)
    return mx_ref.flush(v.astype(BF))
P, K, R = 192, 24, 2
def times(t, v):
    return mx_ref.flush((t.astype(np.float32) * np.asarray(v, np.float32) + np.float32(0)).astype(BF))
def columns(v):
    return mx_ref.flush(np.ascontiguousarray(v.reshape(-1, 128, 4).transpose(1, 0, 2)).reshape(128, -1).astype(np.float32).astype(BF))
def plain(rng):
    return {"x": times(f(rng, N, 128, 4 * P), 64), "u": f(rng, N, 128, 4), "w": f(rng, N, 128, 512)}
def setup_inputs(rng):
    return plain(rng)
def setup_inputs_shadow(rng):
    d, H, xs, us = plain(rng), K // 2, [], []
    for r in range(N):
        way = rng.choice([-1.0, 1.0], 512)
        q = np.where(np.arange(512) < 480, way, 0.0)
        q[480], q[481] = 2.0 ** -14, 2.0 ** -16
        line, at = rng.permutation(480), rng.permutation(P)
        v = rng.standard_normal((P, 512)) * 2.0 ** -4
        v[at[:3 * H + 4 + K]] = 0
        for e, level in ((np.sort(at[:H]), 1.0), (np.sort(at[H:2 * H + 4]), 0.875), (at[2 * H + 4:3 * H + 4], 0.75)):
            for g, j in enumerate(e):
                k = line[16 * (g % H):16 * (g % H) + 16]
                v[j, k] = level * way[k]
                if level > 0.75: v[j, 480], v[j, 481] = 0.25 * (g // 4), 0.25 * (g % 4)
        for j in at[3 * H + 4:3 * H + 4 + K]:
            k = line[16 * H + rng.permutation(480 - 16 * H)[:16]]
            v[j, k] = 0.625 * way[k]
        v = v * rng.choice([-1.0, 1.0], (P, 1))
        xs.append(columns(v * np.exp2(rng.integers(4, 9))))
        us.append(columns(q[None] * np.exp2(rng.integers(-3, 4))))
    return {**d, "x": np.stack(xs), "u": np.stack(us)}
def setup_inputs_ties(rng):
    d = plain(rng)
    d["x"] = np.stack([times(cols(d["x"][r], rng.permutation(np.arange(P) % 6)), np.repeat(rng.choice([-1.0, 1.0], P), 4)) for r in range(N)])
    return d
def setup_inputs_few(rng):
    d = plain(rng)
    n = 8 * rng.integers(K // 8, R * K // 8, N) + rng.integers(4, 8, N)
    p = rng.permutation(N)
    n[p[0]], n[p[1]] = 3, P
    d["x"] = np.stack([times(d["x"][r], 2.0 ** -14 * np.repeat(rng.permutation(P) < n[r], 4)) for r in range(N)])
    return d
def setup_inputs_huge(rng):
    d, xs, us = plain(rng), [], []
    lean = 0.5 + 0.5 * np.sqrt(3.6 / (K - 1))
    for r in range(N):
        way = rng.choice([-1.0, 1.0], 512)
        us.append(columns((way * (1.75 + 0.25 * rng.random(512)) * 2.0 ** 29)[None]))
        v = way * np.where(rng.random((P, 512)) < lean, 1.0, -1.0) * rng.choice([-1.0, 1.0], (P, 1))
        xs.append(columns(v * (1 + rng.random((P, 512))) * 2.0 ** 27))
    return {**d, "x": np.stack(xs), "u": np.stack(us)}
def setup_inputs_spread(rng):
    return {**plain(rng), "x": wide(rng, N, 128, 4 * P, cols=6)}
def check_inputs(d):
    b = []
    for k in ("x", "u", "w"):
        v = np.abs(d[k].astype(np.float32))
        if not (np.isfinite(v).all() and ((v == 0) | (v >= 2.0 ** -30) & (v <= 2.0 ** 30)).all()): b.append("a value of " + k)
    return b
UP = 2.0 ** np.arange(-64, 74)
DOWN = 2.0 ** -np.arange(-64.0, 74)
def play(x, u):
    ask = [mx_ref.quantize(np.concatenate([u[r], np.zeros((128, 508), BF)], axis=1)) for r in range(N)]
    X = mx_ref.quantize(np.concatenate([x[r] for r in range(N)], axis=1))
    free, rounds = np.ones((N, P), bool), []
    for t in range(R):
        at, took = np.full(128, -1), np.zeros((N, K), int)
        for r in range(N):
            s = np.abs(mx_ref.matmul(ask[r], pick(X, P * r + np.arange(P)))[0])
            o = np.argsort(np.where(free[r], 0.0 - s, np.inf), kind="stable")[:K]
            free[r, o] = False
            at[r * K:r * K + K] = P * r + o
            took[r] = o
        m = pick(X, at)
        rounds.append((took, m))
        d = np.diagonal(mx_ref.matmul(m, m))
        h = np.where(d > 0, DOWN[np.maximum(np.searchsorted(UP, d, side="right") - 1, 0)], 0.0).astype(np.float32)
        c = np.zeros((128, N * P, 4), np.float32)
        c[:, :, 0] = mx_ref.matmul(m, X) * h[:, None]
        c = mx_ref.quantize(c.reshape(128, -1).astype(BF))
        dx, parts = decode(X).reshape(128, N * P, 4), []
        dm = np.concatenate([dx, np.zeros((128, 1, 4), np.float32)], axis=1)[:, at]
        for b in range(4):
            mt = np.zeros((128, 128, 4), np.float32)
            mt[:, :, 0] = dm[:, :, b].T
            z = mx_ref.matmul(mx_ref.quantize(mt.reshape(128, 512).astype(BF)), c)
            parts.append(dx[:, :, b] - np.float32(0.25) * z)
        X = mx_ref.quantize(tile(parts))
    return X, rounds
def reference(x, u, w):
    y, pl = np.zeros((N, 128, R * N * K), np.float32), np.zeros((N, 1, R * K), np.float32)
    oc, osc = np.zeros((N, 128, 4 * P), np.uint8), np.zeros((N, 16, P), np.uint8)
    own = [mx_ref.quantize(np.ascontiguousarray(w[r])) for r in range(N)]
    X, rounds = play(x, u)
    for t in range(R):
        took, m = rounds[t]
        for r in range(N):
            pl[r, 0, t * K:t * K + K] = took[r]
            y[r, :, t * N * K:(t + 1) * N * K] = mx_ref.matmul(own[r], m)[:, :N * K]
    for r in range(N):
        oc[r], osc[r] = emit(pick(X, P * r + np.arange(P)))
    return {"y": y, "pl": pl, "oc": oc, "osc": osc}

@@ -1,0 +1,288 @@
+from concourse.bass import DstId, RemoteDMATransfer
+from concourse.mybir import dt, AluOpType, AxisListType, ActivationFunctionType
+
+P, K, R, N = 192, 24, 2, 4
+GAP = 512.0
+NPOW = 136
+Q4, U8, BF, F32 = "float8_e4m3fn_x4", "uint8", "bfloat16", "float32"
+
+SCRATCH = {"pu": ("psum", [128, 1536], F32), "px": ("psum", [128, 2048], F32), "py": ("psum", [128, 512], F32)}
+for _n, _w in (("xt", 4 * P), ("ut", 4), ("wt", 512), ("zer", 512), ("ub", 512), ("kt", 512), ("ct", 4 * P), ("tri", 128),
+               ("dd", P), ("et", 520), ("mt", 2048), ("gt", 4 * P), ("rt", 4 * P), ("up", NPOW), ("two", NPOW), ("fac", NPOW)):
+    SCRATCH[_n] = ("sbuf", [128, _w], BF)
+for _n, _w in (("dig", 2 * P), ("ar", P), ("na", 2), ("plf", 2 * R), ("fr", 2), ("dm", N * K), ("dv", 1), ("hs", NPOW),
+               ("ys", R * N * K)):
+    SCRATCH[_n] = ("sbuf", [128, _w], F32)
+for _n, _w in (("u", 128), ("w", 128), ("k0", 256), ("k1", 256), ("c", P), ("e", 512), ("mt", 512), ("g", P),
+               ("x0", P), ("x1", P), ("x2", P), ("l0", 32), ("l1", 32), ("m0", 224), ("m1", 224)):
+    SCRATCH[_n + "q"] = ("sbuf", [128, _w], Q4)
+    SCRATCH[_n + "s"] = ("sbuf", [128, _w], U8)
+for _t in range(R):
+    SCRATCH["off%d" % _t] = ("sbuf", [128, 2], "uint16")
+NSEM = 145
+SEMAPHORES = ["arr0", "arr1", "snd", "out"] + ["s%d" % _i for _i in range(NSEM)]
+
+
+def reg(name, c0, c1, step=1, p0=0, p1=128):
+    return (name, c0, c1, step, p0, p1)
+
+
+def _meets(a, b):
+    if a[0] != b[0] or a[5] <= b[4] or b[5] <= a[4]:
+        return False
+    return not set(range(a[1], a[2], a[3])).isdisjoint(range(b[1], b[2], b[3]))
+
+
+def emit(ops, queues, T):
+    known = {q: set() for q in queues}
+    for i, o in enumerate(ops):
+        deps = set(o["after"])
+        o["banks"] = set((a[0], a[1] // 512) for a in o["r"] + o["w"] if SCRATCH[a[0]][0] == "psum")
+        for j, e in enumerate(ops[:i]):
+            if j != o["acc"] and (any(_meets(a, b) for a in o["w"] for b in e["r"] + e["w"])
+                                  or any(_meets(a, b) for a in o["r"] for b in e["w"])
+                                  or (e["q"] != o["q"] and o["banks"] & e["banks"])):
+                deps.add(j)
+        o["waits"], o["done"] = [], {i}
+        if o["q"] is not None:
+            for j in sorted(deps, reverse=True):
+                if j not in known[o["q"]]:
+                    o["waits"].insert(0, j)
+                    known[o["q"]] |= ops[j]["done"]
+                    ops[j]["by"].append(i)
+            o["done"] = known[o["q"]] | {i} | (ops[o["acc"]]["done"] if o["acc"] is not None else set())
+    pool = []
+    for i, o in enumerate(ops):
+        if o["q"] is None:
+            continue
+        for j in o["waits"]:
+            queues[o["q"]].wait_ge(*ops[j]["sem"])
+        ins = o["fn"]()
+        if o["sem"] is not None:
+            ins.then_inc(o["sem"], o["inc"])
+        if o["by"]:
+            if len(pool) < NSEM:
+                pool.append([T.sem["s%d" % len(pool)], 0, i])
+                s = pool[-1]
+            else:
+                s = [e for e in pool if ops[e[2]]["inc"] == o["inc"] and e[2] in o["done"] and all(
+                    w in o["done"] or (ops[w]["q"] == o["q"] and w < i) for w in ops[e[2]]["by"])][0]
+            s[1], s[2] = s[1] + o["inc"], i
+            o["sem"] = (s[0], s[1])
+            ins.then_inc(s[0], o["inc"])
+
+
+def rank_program(g, core, T, topo):
+    rank = T.rank_of(core)
+    if rank is None:
+        return
+    A, F = AluOpType, ActivationFunctionType
+    V, S, PE, Y = g.vector, g.scalar, g.tensor, g.sync
+    queues = {"g": g, "v": V, "s": S, "t": PE, "y": Y}
+    ops, own = [], []
+
+    def ap(a):
+        return T[a[0]][a[4]:a[5], a[1]:a[2]:a[3]] if a[3] != 1 else T[a[0]][a[4]:a[5], a[1]:a[2]]
+
+    def val(a):
+        return ap(a) if isinstance(a, tuple) else a
+
+    def op(q, fn, r=(), w=(), after=(), acc=None, inc=1, sem=None):
+        ops.append({"q": q, "fn": fn, "r": [a for a in r if isinstance(a, tuple)], "w": list(w), "after": list(after),
+                    "acc": acc, "inc": inc, "by": [], "sem": sem})
+        return len(ops) - 1
+
+    def pair(name, c0, c1):
+        return reg(name + "q", c0, c1), reg(name + "s", c0, c1)
+
+    def fill(out, c):
+        op("v", lambda: V.memset(ap(out), c), w=[out])
+
+    def quant(name, c0, n, src, s0=0):
+        (cq, cs), t = pair(name, c0, c0 + n), reg(src, s0, s0 + 4 * n)
+        op("v", lambda: V.quantize_mx(ap(cq), ap(cs), ap(t)), r=[t], w=[cq, cs])
+
+    def mm(out, lhs, rhs, start=True, stop=True, acc=None):
+        return op("t", lambda: PE.matmul_mx(ap(out), ap(lhs[0]), ap(lhs[1]), ap(rhs[0]), ap(rhs[1]), start, stop),
+                  r=list(lhs) + list(rhs), w=[out], acc=acc)
+
+    def ts(out, in0, s1, op0, s2=None, *op1):
+        op("v", lambda: V.tensor_scalar(ap(out), ap(in0), val(s1), s2, op0, *op1), r=[in0, s1], w=[out])
+
+    def tt(out, in0, in1, o):
+        op("v", lambda: V.tensor_tensor(ap(out), ap(in0), ap(in1), o), r=[in0, in1], w=[out])
+
+    def cp(out, in_):
+        op("v", lambda: V.tensor_copy(ap(out), ap(in_)), r=[in_], w=[out])
+
+    def red(out, in_, o, neg=False, size=False):
+        op("v", lambda: V.tensor_reduce(ap(out), ap(in_), AxisListType.X, o, negate=neg, apply_absolute_value=size),
+           r=[in_], w=[out])
+
+    def scan(out, d0, d1, first):
+        op("v", lambda: V.tensor_tensor_scan(ap(out), ap(d0), ap(d1), first, A.mult, A.add), r=[d0, d1], w=[out])
+
+    def act(out, in_, f, bias=0.0, scale=1.0):
+        op("s", lambda: S.activation(ap(out), ap(in_), f, bias=val(bias), scale=val(scale)), r=[in_, bias, scale], w=[out])
+
+    def iota(out, pattern):
+        own.append(op("g", lambda: g.iota(ap(out), pattern, 0, 0, allow_small_or_imprecise_dtypes=True), w=[out], after=own[-1:]))
+
+    def sel(out, in_, cmp, c):
+        own.append(op("g", lambda: g.affine_select(ap(out), ap(in_), [[-1, 128]], cmp, c, 0, 1), r=[in_], w=[out], after=own[-1:]))
+
+    def dma(q, out, in_, r=(), w=(), after=(), sem=None):
+        op(q, lambda: queues[q].dma_start(out(), in_()), r=r, w=w, after=after, inc=16, sem=sem)
+
+    def pick(dst, n, src, width, off):
+        (dq, ds), (sq, ss) = pair(dst, 0, n), pair(src, 0, width)
+        op("v", lambda: V.tensor_copy(ap(dq).bitcast(dt.uint32), ap(sq).bitcast(dt.uint32).indirect(ap(off))),
+           r=[sq, off], w=[dq])
+        op("s", lambda: S.activation(ap(ds), ap(ss).indirect(ap(off)), F.Copy), r=[ss, off], w=[ds])
+
+    peers = [c for c in T.cores if c != core]
+    far = [c for c in peers if topo.chip(c) != topo.chip(core)]
+    near = [c for c in peers if topo.chip(c) == topo.chip(core)]
+    outer = topo.engines(core, far[0])
+    inner = [e for e in topo.engines(core, near[0]) if e not in outer]
+    per = len(outer) // len(far)
+    lanes = {c: outer[i * per:(i + 1) * per] for i, c in enumerate(far)}
+    spread = inner[::len(inner) // (per * len(near))]
+    lanes.update({c: spread[i * per:(i + 1) * per] for i, c in enumerate(near)})
+    count = 2 * per * len(peers)
+
+    def send(t):
+        src, dst = pair("l%d" % t, 0, K), pair("m%d" % t, K * rank, K * rank + K)
+        for h in range(2):
+            side = (lambda a: ap(a).bitcast(dt.uint8)) if h == 0 else ap
+
+            def go(h=h, side=side):
+                trs = []
+                for c in far + near:
+                    rid, pid = topo.addr(c)[:2]
+                    trs.append(RemoteDMATransfer(dst_ids=[DstId(rid=rid, pnc=pid)], dma_engine_mask=sum(1 << e for e in lanes[c]),
+                                                 remote_sem=T.sem["arr%d" % t], src=side(src[h]), dst=side(dst[h])))
+                return g.remote_dma_fused(trs, local_sem=T.sem.snd)
+            op("g", go, r=[src[h]])
+            dma("ys"[h], lambda h=h, side=side: side(dst[h]), lambda h=h, side=side: side(src[h]), r=[src[h]], w=[dst[h]])
+        land = []
+        for c in peers:
+            land += pair("m%d" % t, K * T.rank_of(c), K * T.rank_of(c) + K)
+        op(None, None, w=land, sem=(T.sem["arr%d" % t], count))
+
+    zer = lambda n, p0=0, p1=128: reg("zer", 0, n, 1, p0, p1)
+    bank = lambda name, b, n, p0=0, p1=128: reg(name, 512 * b, 512 * b + n, 1, p0, p1)
+
+    dma("y", lambda: T.xt[:], lambda: T.x[:], w=[reg("xt", 0, 4 * P)])
+    dma("s", lambda: T.ut[:], lambda: T.u[:], w=[reg("ut", 0, 4)])
+    fill(reg("kt", 0, 512), GAP)
+    fill(zer(512), 0.0)
+    iota(reg("dig", 0, 2 * P, 2, 0, 1), [[0, P // 16], [1, 16]])
+    iota(reg("kt", 1, 512, 4, 32, 33), [[0, 8], [-int(GAP), 16]])
+    iota(reg("dig", 1, 2 * P, 2, 0, 1), [[16, P // 16], [0, 16]])
+    sel(reg("tri", 0, 128), zer(128), A.is_ge, 2.0 ** -110)
+    fill(reg("kt", 2, 512, 4, 0, 64), 0.0)
+    fill(reg("kt", 3, 512, 4, 32, 33), 0.0)
+    fill(reg("et", 0, 520), 0.0)
+    for b in range(4):
+        dma("y", lambda b=b: T.mt[:, 512 * b:512 * b + 512], lambda: T.zer[:], r=[zer(512)], w=[reg("mt", 512 * b, 512 * b + 512)])
+    dma("y", lambda: T.wt[:], lambda: T.w[:], w=[reg("wt", 0, 512)])
+    act(reg("ct", 1, 4 * P, 2), zer(2 * P), F.Copy)
+    act(reg("ct", 1, 4 * P, 2, 32, 33), zer(2 * P, 32, 33), F.Identity, 1.0)
+    quant("k0", 0, 128, "kt")
+    fill(reg("kt", 3, 512, 4, 32, 33), -16 * GAP)
+    quant("k0", 128, 128, "kt")
+    for b in range(2):
+        ts(reg("ub", b, 512, 4), zer(128), reg("ut", b, b + 1), A.add)
+        act(reg("ub", b + 2, 512, 4), zer(128), F.Identity, reg("ut", b + 2, b + 3))
+    quant("u", 0, 128, "ub")
+    quant("x0", 0, P, "xt")
+    act(reg("ct", 1, 4 * P, 2, 0, 1), reg("dig", 0, 2 * P, 1, 0, 1), F.Copy, scale=1.0 / GAP)
+    sel(reg("et", 3, 515, 4), zer(128), A.not_equal, 1.0)
+
+    naA, naB = reg("na", 0, 1), reg("na", 1, 2)
+    for t in range(R):
+        x, nx, kk, m = "x%d" % t, "x%d" % (t + 1), "k%d" % t, "m%d" % t
+        off = reg("off%d" % t, 0, 2)
+        mm(bank("pu", 0, P), pair("u", 0, 128), pair(x, 0, P))
+        mm(bank("pu", 1, 128), pair(x, 0, 128), pair("u", 0, 128))
+        mm(bank("pu", 2, 128), pair(x, 64, P), pair("u", 0, 128))
+        act(reg("ar", 0, P), bank("pu", 0, P), F.Abs)
+        red(naA, bank("pu", 1, 1), A.max, True, True)
+        red(naB, bank("pu", 2, 1), A.max, True, True)
+        act(reg("dd", 0, 128), reg("ar", 0, 128), F.Identity, naA)
+        act(reg("dd", 128, P), reg("ar", 128, P), F.Identity, naB)
+        ts(reg("ct", 2, 512, 4), reg("ar", 0, 128), naB, A.add, 0.0, A.is_lt)
+        ts(reg("ct", 512, 4 * P, 4), reg("ar", 128, P), naA, A.add, 0.0, A.is_le)
+        tt(reg("ct", 0, 512, 4), reg("dd", 0, 128), reg("tri", 0, 128), A.is_lt)
+        tt(reg("ct", 514, 4 * P, 4), reg("dd", 128, P), reg("tri", 64, 128), A.is_lt)
+        quant("c", 0, P, "ct")
+        for c in range(2):
+            mm(bank("pu", 1 + c, P), pair(kk, 128 * c, 128 * c + 128), pair("c", 0, P))
+        for c in range(2):
+            red(reg("plf", 2 * t + c, 2 * t + c + 1), bank("pu", 1 + c, P), A.min, False, True)
+        cp(off, reg("plf", 2 * t, 2 * t + 2))
+        pick("l%d" % t, 32, x, P, off)
+        send(t)
+
+        quant(m, N * K, 128, "zer")
+        if t == 0:
+            act(reg("gt", 0, 512), zer(512), F.Copy)
+            act(reg("gt", 512, 4 * P), zer(4 * P - 512), F.Copy)
+            for b in range(4):
+                quant("e", 128 * b, 128, "et", 3 - b)
+            fill(reg("two", 0, NPOW), 2.0)
+            quant("w", 0, 128, "wt")
+            scan(reg("up", 0, NPOW), reg("two", 0, NPOW), zer(NPOW), 2.0 ** -64)
+        if t + 1 < R:
+            mm(bank("pu", 0, 128), pair("c", 0, 128), pair(kk, 0, 128))
+            mm(bank("pu", 2, 128), pair("c", 64, P), pair(kk, 0, 128))
+            ts(reg("ct", 1, 4 * P, 4, 64, 65), bank("pu", 1, P, 64, 65), K * GAP, A.is_lt, 256.0, A.mult)
+            ts(reg("fr", 0, 1), bank("pu", 0, 1), K * GAP, A.is_ge)
+            ts(reg("fr", 1, 2), bank("pu", 2, 1), K * GAP, A.is_ge)
+            for c in range(2):
+                ts(reg("kt", 2 * c, 512, 4), reg("kt", 2 * c, 512, 4), reg("fr", c, c + 1), A.mult)
+            quant("k%d" % (t + 1), 128, 128, "kt")
+            fill(reg("kt", 3, 512, 4, 32, 33), 0.0)
+            quant("k%d" % (t + 1), 0, 128, "kt")
+
+        M = pair(m, 0, 128)
+        got = mm(bank("px", 0, 128), M, M)
+        mm(bank("px", 1, 256), M, pair("e", 0, 256))
+        mm(bank("px", 2, 256), M, pair("e", 256, 512))
+        mm(bank("px", 3, P), M, pair(x, 0, P))
+        mm(bank("py", 0, 128), pair("w", 0, 128), M)
+        tt(reg("dm", 0, N * K), bank("px", 0, N * K), reg("et", 3, 3 + 4 * N * K, 4), A.mult)
+        act(reg("mt", 0, 1024, 4), bank("px", 1, 256), F.Copy)
+        act(reg("mt", 1024, 2048, 4), bank("px", 2, 256), F.Copy)
+        red(reg("dv", 0, 1), reg("dm", 0, N * K), A.max)
+        ts(reg("fac", 0, NPOW), reg("up", 0, NPOW), reg("dv", 0, 1), A.is_gt, 0.5, A.max)
+        scan(reg("hs", 0, NPOW), reg("fac", 0, NPOW), zer(NPOW), -0.25 * 2.0 ** 64)
+        act(reg("gt", 0, 4 * P, 4), bank("px", 3, P), F.Copy, scale=reg("hs", NPOW - 1, NPOW))
+        quant("mt", 0, 256, "mt")
+        d = [mm(bank("px", b, P), pair("e", 128 * b, 128 * b + 128), pair(x, 0, P), True, False) for b in range(4)]
+        quant("g", 0, P, "gt")
+        act(reg("ys", t * N * K, (t + 1) * N * K), bank("py", 0, N * K), F.Copy)
+        quant("mt", 256, 256, "mt", 1024)
+        for b in range(4):
+            mm(bank("px", b, P), pair("mt", 128 * b, 128 * b + 128), pair("g", 0, P), False, True, acc=d[b])
+        for b in range(4):
+            if b % 2:
+                cp(reg("rt", b, 4 * P, 4), bank("px", b, P))
+            else:
+                act(reg("rt", b, 4 * P, 4), bank("px", b, P), F.Copy)
+        quant(nx, 0, P, "rt")
+
+    last, out = "x%d" % R, T.sem.out
+    for t in range(R):
+        for c, n in ((0, 16), (1, K - 16)):
+            a = reg("plf", 2 * t + c, 2 * t + c + 1, 1, 0, n)
+            dma("y", lambda t=t, c=c, n=n: T.pl[0:1, K * t + 16 * c:K * t + 16 * c + n], lambda a=a: ap(a), r=[a], after=[got], sem=out)
+    dma("y", lambda: T.y[:], lambda: T.ys[:], r=[reg("ys", 0, R * N * K)], sem=out)
+    dma("y", lambda: T.oc[:], lambda: T[last + "q"][:].bitcast(dt.uint8), r=[reg(last + "q", 0, P)], sem=out)
+    for k in range(4):
+        a = reg(last + "s", 0, P, 1, 32 * k, 32 * k + 4)
+        dma("s" if k < 2 else "y", lambda k=k: T.osc[4 * k:4 * k + 4, :], lambda a=a: ap(a), r=[a], sem=out)
+    emit(ops, queues, T)
+    Y.wait_ge(out, 16 * (2 * R + 6))
+    g.wait_ge(T.sem.snd, R * count)

@@ -2,19 +2,20 @@ from concourse.bass import DstId, RemoteDMATransfer
 from concourse.mybir import dt, AluOpType, AxisListType, ActivationFunctionType
 
 P, K, R, N = 192, 24, 2, 4
+LAY = (N - 1) * K
 GAP = 512.0
 NPOW = 136
 Q4, U8, BF, F32 = "float8_e4m3fn_x4", "uint8", "bfloat16", "float32"
 
-SCRATCH = {"pu": ("psum", [128, 1536], F32), "px": ("psum", [128, 2048], F32), "py": ("psum", [128, 512], F32)}
-for _n, _w in (("xt", 4 * P), ("ut", 4), ("wt", 512), ("zer", 512), ("ub", 512), ("kt", 512), ("ct", 4 * P), ("tri", 128),
-               ("dd", P), ("et", 520), ("mt", 2048), ("gt", 4 * P), ("rt", 4 * P), ("up", NPOW), ("two", NPOW), ("fac", NPOW)):
+SCRATCH = {"pu": ("psum", [128, 1536], F32), "px": ("psum", [128, 2048], F32), "pr": ("psum", [128, 512], F32)}
+for _n, _w in (("xt", 4 * P), ("ut", 4), ("wt", 512), ("zer", 512), ("ub", 512), ("kt", 512), ("ct", 4 * P),
+               ("dd", P), ("dig", P), ("et", 524), ("mt", 2048), ("gt", 4 * P), ("rt", 4 * P), ("up", NPOW), ("two", NPOW),
+               ("fac", NPOW), ("hs", NPOW), ("gb", P)):
     SCRATCH[_n] = ("sbuf", [128, _w], BF)
-for _n, _w in (("dig", 2 * P), ("ar", P), ("na", 2), ("plf", 2 * R), ("fr", 2), ("dm", N * K), ("dv", 1), ("hs", NPOW),
-               ("ys", R * N * K)):
+for _n, _w in (("ar", P), ("na", 2), ("plf", R), ("fr", 2), ("dm", N * K), ("dv", 1), ("ys", R * N * K), ("dx", 2 * P)):
     SCRATCH[_n] = ("sbuf", [128, _w], F32)
-for _n, _w in (("u", 128), ("w", 128), ("k0", 256), ("k1", 256), ("c", P), ("e", 512), ("mt", 512), ("g", P),
-               ("x0", P), ("x1", P), ("x2", P), ("l0", 32), ("l1", 32), ("m0", 224), ("m1", 224)):
+for _n, _w in (("u", 128), ("w", 128), ("k0", 128), ("k1", 128), ("c", P), ("e", 512), ("mt", 512), ("g", P),
+               ("x0", P + 128), ("x1", P), ("x2", P), ("l0", 32), ("l1", 224), ("m0", 224), ("m1", 224)):
     SCRATCH[_n + "q"] = ("sbuf", [128, _w], Q4)
     SCRATCH[_n + "s"] = ("sbuf", [128, _w], U8)
 for _t in range(R):
@@ -50,26 +51,27 @@ def emit(ops, queues, T):
                     o["waits"].insert(0, j)
                     known[o["q"]] |= ops[j]["done"]
                     ops[j]["by"].append(i)
+            o["waits"].sort(key=lambda j: ops[j]["q"] is None)
             o["done"] = known[o["q"]] | {i} | (ops[o["acc"]]["done"] if o["acc"] is not None else set())
-    pool = []
+    teams = {}
     for i, o in enumerate(ops):
+        if o["q"] is not None and o["by"]:
+            teams.setdefault((o["inc"], tuple(o["by"])), []).append(i)
+    for n, team in enumerate(teams.values()):
+        both = (T.sem["s%d" % n], ops[team[0]]["inc"] * len(team))
+        for j in team:
+            ops[j]["sem"] = both
+    for o in ops:
         if o["q"] is None:
             continue
+        seen = []
         for j in o["waits"]:
-            queues[o["q"]].wait_ge(*ops[j]["sem"])
+            if not any(ops[j]["sem"] is s for s in seen):
+                seen.append(ops[j]["sem"])
+                queues[o["q"]].wait_ge(*ops[j]["sem"])
         ins = o["fn"]()
         if o["sem"] is not None:
-            ins.then_inc(o["sem"], o["inc"])
-        if o["by"]:
-            if len(pool) < NSEM:
-                pool.append([T.sem["s%d" % len(pool)], 0, i])
-                s = pool[-1]
-            else:
-                s = [e for e in pool if ops[e[2]]["inc"] == o["inc"] and e[2] in o["done"] and all(
-                    w in o["done"] or (ops[w]["q"] == o["q"] and w < i) for w in ops[e[2]]["by"])][0]
-            s[1], s[2] = s[1] + o["inc"], i
-            o["sem"] = (s[0], s[1])
-            ins.then_inc(s[0], o["inc"])
+            ins.then_inc(o["sem"][0] if o["by"] else o["sem"], o["inc"])
 
 
 def rank_program(g, core, T, topo):
@@ -83,6 +85,9 @@ def rank_program(g, core, T, topo):
 
     def ap(a):
         return T[a[0]][a[4]:a[5], a[1]:a[2]:a[3]] if a[3] != 1 else T[a[0]][a[4]:a[5], a[1]:a[2]]
+
+    def raw(a):
+        return ap(a).bitcast(dt.uint8) if SCRATCH[a[0]][2] == Q4 else ap(a)
 
     def val(a):
         return ap(a) if isinstance(a, tuple) else a
@@ -119,8 +124,8 @@ def rank_program(g, core, T, topo):
         op("v", lambda: V.tensor_reduce(ap(out), ap(in_), AxisListType.X, o, negate=neg, apply_absolute_value=size),
            r=[in_], w=[out])
 
-    def scan(out, d0, d1, first):
-        op("v", lambda: V.tensor_tensor_scan(ap(out), ap(d0), ap(d1), first, A.mult, A.add), r=[d0, d1], w=[out])
+    def scan(out, d0, d1, first, o=A.mult):
+        op("v", lambda: V.tensor_tensor_scan(ap(out), ap(d0), ap(d1), first, o, A.add), r=[d0, d1], w=[out])
 
     def act(out, in_, f, bias=0.0, scale=1.0):
         op("s", lambda: S.activation(ap(out), ap(in_), f, bias=val(bias), scale=val(scale)), r=[in_, bias, scale], w=[out])
@@ -132,10 +137,10 @@ def rank_program(g, core, T, topo):
         own.append(op("g", lambda: g.affine_select(ap(out), ap(in_), [[-1, 128]], cmp, c, 0, 1), r=[in_], w=[out], after=own[-1:]))
 
     def dma(q, out, in_, r=(), w=(), after=(), sem=None):
-        op(q, lambda: queues[q].dma_start(out(), in_()), r=r, w=w, after=after, inc=16, sem=sem)
+        return op(q, lambda: queues[q].dma_start(out(), in_()), r=r, w=w, after=after, inc=16, sem=sem)
 
-    def pick(dst, n, src, width, off):
-        (dq, ds), (sq, ss) = pair(dst, 0, n), pair(src, 0, width)
+    def pick(dst, c0, n, src, width, off):
+        (dq, ds), (sq, ss) = pair(dst, c0, c0 + n), pair(src, 0, width)
         op("v", lambda: V.tensor_copy(ap(dq).bitcast(dt.uint32), ap(sq).bitcast(dt.uint32).indirect(ap(off))),
            r=[sq, off], w=[dq])
         op("s", lambda: S.activation(ap(ds), ap(ss).indirect(ap(off)), F.Copy), r=[ss, off], w=[ds])
@@ -152,137 +157,175 @@ def rank_program(g, core, T, topo):
     count = 2 * per * len(peers)
 
     def send(t):
-        src, dst = pair("l%d" % t, 0, K), pair("m%d" % t, K * rank, K * rank + K)
+        src, dst = pair("l%d" % t, LAY * t, LAY * t + K), pair("m%d" % t, K * rank, K * rank + K)
         for h in range(2):
-            side = (lambda a: ap(a).bitcast(dt.uint8)) if h == 0 else ap
-
-            def go(h=h, side=side):
+            def go(h=h):
                 trs = []
                 for c in far + near:
                     rid, pid = topo.addr(c)[:2]
                     trs.append(RemoteDMATransfer(dst_ids=[DstId(rid=rid, pnc=pid)], dma_engine_mask=sum(1 << e for e in lanes[c]),
-                                                 remote_sem=T.sem["arr%d" % t], src=side(src[h]), dst=side(dst[h])))
+                                                 remote_sem=T.sem["arr%d" % t], src=raw(src[h]), dst=raw(dst[h])))
                 return g.remote_dma_fused(trs, local_sem=T.sem.snd)
             op("g", go, r=[src[h]])
-            dma("ys"[h], lambda h=h, side=side: side(dst[h]), lambda h=h, side=side: side(src[h]), r=[src[h]], w=[dst[h]])
-        land = []
-        for c in peers:
-            land += pair("m%d" % t, K * T.rank_of(c), K * T.rank_of(c) + K)
-        op(None, None, w=land, sem=(T.sem["arr%d" % t], count))
+            if t == 0:
+                dma("y", lambda h=h: raw(dst[h]), lambda h=h: raw(src[h]), r=[src[h]], sem=T.sem["arr%d" % t])
+        land = [a for c in range(N) if t == 0 or c != rank for a in pair("m%d" % t, K * c, K * c + K)]
+        op(None, None, w=land, sem=(T.sem["arr%d" % t], count + 32 * (1 - t)))
 
     zer = lambda n, p0=0, p1=128: reg("zer", 0, n, 1, p0, p1)
     bank = lambda name, b, n, p0=0, p1=128: reg(name, 512 * b, 512 * b + n, 1, p0, p1)
 
     dma("y", lambda: T.xt[:], lambda: T.x[:], w=[reg("xt", 0, 4 * P)])
     dma("s", lambda: T.ut[:], lambda: T.u[:], w=[reg("ut", 0, 4)])
-    fill(reg("kt", 0, 512), GAP)
     fill(zer(512), 0.0)
-    iota(reg("dig", 0, 2 * P, 2, 0, 1), [[0, P // 16], [1, 16]])
-    iota(reg("kt", 1, 512, 4, 32, 33), [[0, 8], [-int(GAP), 16]])
-    iota(reg("dig", 1, 2 * P, 2, 0, 1), [[16, P // 16], [0, 16]])
-    sel(reg("tri", 0, 128), zer(128), A.is_ge, 2.0 ** -110)
-    fill(reg("kt", 2, 512, 4, 0, 64), 0.0)
-    fill(reg("kt", 3, 512, 4, 32, 33), 0.0)
-    fill(reg("et", 0, 520), 0.0)
-    for b in range(4):
-        dma("y", lambda b=b: T.mt[:, 512 * b:512 * b + 512], lambda: T.zer[:], r=[zer(512)], w=[reg("mt", 512 * b, 512 * b + 512)])
+    fill(reg("et", 0, 524), 0.0)
+    iota(reg("dig", 0, P, 1, 0, 64), [[0, P // 16], [1, 16]])
+    act(reg("ct", 1, 4 * P, 2), zer(2 * P), F.Identity, 1.0)
+    sel(reg("et", 7, 519, 4), zer(128), A.not_equal, 1.0)
+    iota(reg("ct", 3, 4 * P, 4, 0, 1), [[16, P // 16], [0, 16]])
+    for a in [reg("gt", 512, 4 * P)] + [reg("mt", 512 * b, 512 * b + 512) for b in range(4)]:
+        dma("y", lambda a=a: ap(a), lambda a=a: ap(zer(a[2] - a[1])), r=[zer(512)], w=[a])
     dma("y", lambda: T.wt[:], lambda: T.w[:], w=[reg("wt", 0, 512)])
-    act(reg("ct", 1, 4 * P, 2), zer(2 * P), F.Copy)
-    act(reg("ct", 1, 4 * P, 2, 32, 33), zer(2 * P, 32, 33), F.Identity, 1.0)
-    quant("k0", 0, 128, "kt")
-    fill(reg("kt", 3, 512, 4, 32, 33), -16 * GAP)
-    quant("k0", 128, 128, "kt")
-    for b in range(2):
+    fill(reg("gt", 1, 512, 2), 0.0)
+    fill(reg("kt", 1, 512, 2), 0.0)
+    act(reg("gt", 2, 512, 4), zer(128), F.Copy)
+    act(reg("kt", 2, 512, 4, 0, 64), zer(128, 0, 64), F.Copy)
+    fill(reg("kt", 0, 512, 4), GAP)
+    fill(reg("kt", 2, 512, 4, 64, 128), GAP)
+    for b in range(3):
         ts(reg("ub", b, 512, 4), zer(128), reg("ut", b, b + 1), A.add)
-        act(reg("ub", b + 2, 512, 4), zer(128), F.Identity, reg("ut", b + 2, b + 3))
+    act(reg("ub", 3, 512, 4), zer(128), F.Identity, reg("ut", 3, 4))
+    act(reg("kt", 1, 512, 4, 32, 33), reg("dig", 0, 128, 1, 32, 33), F.Copy, scale=-GAP)
+    act(reg("kt", 259, 512, 4, 32, 33), zer(64, 32, 33), F.Identity, -16 * GAP)
+    act(reg("kt", 1, 512, 2, 0, 1), zer(256, 0, 1), F.Identity, 1.0)
+    act(reg("ct", 1, 4 * P, 4, 0, 1), reg("dig", 0, P, 1, 0, 1), F.Copy)
+    scan(reg("gt", 0, 512, 4), zer(128), reg("et", 3, 515, 4), 0.0, A.add)
     quant("u", 0, 128, "ub")
     quant("x0", 0, P, "xt")
-    act(reg("ct", 1, 4 * P, 2, 0, 1), reg("dig", 0, 2 * P, 1, 0, 1), F.Copy, scale=1.0 / GAP)
-    sel(reg("et", 3, 515, 4), zer(128), A.not_equal, 1.0)
 
-    naA, naB = reg("na", 0, 1), reg("na", 1, 2)
+    naA, naB, out = reg("na", 0, 1), reg("na", 1, 2), T.sem.out
+    tri = lambda c0, c1: reg("pr", P + c0, P + c1)
+    into = [bank("px", 1, P), bank("pr", 0, P), bank("px", 2, P), bank("px", 0, P)]
+    slot = lambda name, b: pair(name, 128 * (b ^ 1), 128 * (b ^ 1) + 128)
     for t in range(R):
         x, nx, kk, m = "x%d" % t, "x%d" % (t + 1), "k%d" % t, "m%d" % t
         off = reg("off%d" % t, 0, 2)
+        unpack = lambda b, to, n=P: mm(to, slot("e", b), pair(x, 0, n), True, b % 2 == 0)
+        d = {}
         mm(bank("pu", 0, P), pair("u", 0, 128), pair(x, 0, P))
         mm(bank("pu", 1, 128), pair(x, 0, 128), pair("u", 0, 128))
         mm(bank("pu", 2, 128), pair(x, 64, P), pair("u", 0, 128))
+        if t == 0:
+            quant("e", 128, 128, "et", 7)
+            quant(x, P, 128, "gt")
+            unpack(0, bank("pr", 0, P + 128), P + 128)
+        else:
+            quant("l1", 0, 128, "zer")
+            unpack(0, into[0])
+            unpack(2, into[2])
+        quant(kk, 0, 128, "kt")
         act(reg("ar", 0, P), bank("pu", 0, P), F.Abs)
         red(naA, bank("pu", 1, 1), A.max, True, True)
         red(naB, bank("pu", 2, 1), A.max, True, True)
-        act(reg("dd", 0, 128), reg("ar", 0, 128), F.Identity, naA)
-        act(reg("dd", 128, P), reg("ar", 128, P), F.Identity, naB)
-        ts(reg("ct", 2, 512, 4), reg("ar", 0, 128), naB, A.add, 0.0, A.is_lt)
+        act(reg("dd", 0, 128), reg("ar", 0, 128), F.Sign, naA)
+        act(reg("dd", 128, P), reg("ar", 128, P), F.Sign, naB)
         ts(reg("ct", 512, 4 * P, 4), reg("ar", 128, P), naA, A.add, 0.0, A.is_le)
-        tt(reg("ct", 0, 512, 4), reg("dd", 0, 128), reg("tri", 0, 128), A.is_lt)
-        tt(reg("ct", 514, 4 * P, 4), reg("dd", 128, P), reg("tri", 64, 128), A.is_lt)
+        ts(reg("ct", 2, 512, 4), reg("ar", 0, 128), naB, A.add, 0.0, A.is_lt)
+        tt(reg("ct", 0, 512, 4), reg("dd", 0, 128), tri(0, 128), A.is_lt)
+        tt(reg("ct", 514, 4 * P, 4), reg("dd", 128, P), tri(64, 128), A.is_lt)
+        act(reg("dx", 0, P), into[1 - t], F.Copy)
+        if t == 1:
+            act(reg("dx", P, 2 * P), into[2], F.Copy)
         quant("c", 0, P, "ct")
+        mm(bank("pu", 1, P), pair(kk, 0, 128), pair("c", 0, P))
+        red(reg("plf", t, t + 1), bank("pu", 1, P), A.min, False, True)
         for c in range(2):
-            mm(bank("pu", 1 + c, P), pair(kk, 128 * c, 128 * c + 128), pair("c", 0, P))
-        for c in range(2):
-            red(reg("plf", 2 * t + c, 2 * t + c + 1), bank("pu", 1 + c, P), A.min, False, True)
-        cp(off, reg("plf", 2 * t, 2 * t + 2))
-        pick("l%d" % t, 32, x, P, off)
+            for half in range(2):
+                cp(reg(off[0], c, c + 1, 1, 64 * half, 64 * half + 64), reg("plf", t, t + 1, 1, 64 * c, 64 * c + 64))
+        pick("l%d" % t, LAY * t, 32, x, P, off)
         send(t)
 
-        quant(m, N * K, 128, "zer")
         if t == 0:
-            act(reg("gt", 0, 512), zer(512), F.Copy)
-            act(reg("gt", 512, 4 * P), zer(4 * P - 512), F.Copy)
-            for b in range(4):
-                quant("e", 128 * b, 128, "et", 3 - b)
+            for b in (2, 1, 3):
+                quant("e", 128 * (b ^ 1), 128, "et", 7 - b)
             fill(reg("two", 0, NPOW), 2.0)
-            quant("w", 0, 128, "wt")
+            quant(m, N * K, 128, "zer")
             scan(reg("up", 0, NPOW), reg("two", 0, NPOW), zer(NPOW), 2.0 ** -64)
-        if t + 1 < R:
+            quant("w", 0, 128, "wt")
+            quant("m1", N * K, 128, "zer")
             mm(bank("pu", 0, 128), pair("c", 0, 128), pair(kk, 0, 128))
             mm(bank("pu", 2, 128), pair("c", 64, P), pair(kk, 0, 128))
-            ts(reg("ct", 1, 4 * P, 4, 64, 65), bank("pu", 1, P, 64, 65), K * GAP, A.is_lt, 256.0, A.mult)
-            ts(reg("fr", 0, 1), bank("pu", 0, 1), K * GAP, A.is_ge)
-            ts(reg("fr", 1, 2), bank("pu", 2, 1), K * GAP, A.is_ge)
+            unpack(2, into[2])
+        else:
+            quant("l1", N * K, 128, "zer")
+        d[1] = unpack(1, into[1])
+        if t == 0:
+            act(reg("fr", 0, 1), bank("pu", 0, 1), F.Sign, 256.0 - K * GAP)
+            act(reg("fr", 1, 2), bank("pu", 2, 1), F.Sign, 256.0 - K * GAP)
+            act(reg("dx", P, 2 * P), into[2], F.Copy)
             for c in range(2):
-                ts(reg("kt", 2 * c, 512, 4), reg("kt", 2 * c, 512, 4), reg("fr", c, c + 1), A.mult)
-            quant("k%d" % (t + 1), 128, 128, "kt")
-            fill(reg("kt", 3, 512, 4, 32, 33), 0.0)
-            quant("k%d" % (t + 1), 0, 128, "kt")
+                act(reg("kt", 2 * c, 512, 4), reg("kt", 2 * c, 512, 4), F.Relu, scale=reg("fr", c, c + 1))
+            act(reg("ct", 1, 4 * P, 4, 64, 65), bank("pu", 1, P, 64, 65), F.Relu, 2048.0 * ((K - 16) * GAP - 256.0), -2048.0)
+            fill(reg("kt", 1, 512, 4, 64, 65), 1.0)
 
         M = pair(m, 0, 128)
-        got = mm(bank("px", 0, 128), M, M)
-        mm(bank("px", 1, 256), M, pair("e", 0, 256))
-        mm(bank("px", 2, 256), M, pair("e", 256, 512))
-        mm(bank("px", 3, P), M, pair(x, 0, P))
-        mm(bank("py", 0, 128), pair("w", 0, 128), M)
-        tt(reg("dm", 0, N * K), bank("px", 0, N * K), reg("et", 3, 3 + 4 * N * K, 4), A.mult)
-        act(reg("mt", 0, 1024, 4), bank("px", 1, 256), F.Copy)
+
+        def with_m(a, start, stop, acc):
+            return [mm(bank("px", 0, 128), a, a, start, stop, acc[0]), mm(bank("px", 3, P), a, pair(x, 0, P), start, stop, acc[1]),
+                    mm(bank("px", 1, 256), a, pair("e", 0, 256), start, stop, acc[2]),
+                    mm(bank("px", 2, 256), a, pair("e", 256, 512), start, stop, acc[3])]
+        if t == 0:
+            ya, got = None, with_m(M, True, True, [None] * 4)[0]
+            for a, b in zip(pair("m1", K * rank, K * rank + K), pair("m1", N * K, N * K + K)):
+                dma("y", lambda a=a: raw(a), lambda b=b: raw(b), r=[b], w=[a], after=[got])
+        else:
+            mine = pair("l1", LAY - K * rank, LAY - K * rank + 128)
+            early = with_m(mine, True, False, [None] * 4)
+            ya = mm(bank("pu", 2, 128), pair("w", 0, 128), mine, True, False)
+            got = with_m(M, False, True, early)[0]
+        for c, n in ((0, 16), (1, K - 16)):
+            a = reg("plf", t, t + 1, 1, 64 * c, 64 * c + n)
+            dma("y", lambda t=t, c=c, n=n: T.pl[0:1, K * t + 16 * c:K * t + 16 * c + n], lambda a=a: ap(a), r=[a], after=[got], sem=out)
+        tt(reg("dm", 0, N * K), bank("px", 0, N * K), reg("et", 7, 7 + 4 * N * K, 4), A.mult)
+        act(reg("gb", 0, P), bank("px", 3, P), F.Copy)
+        act(reg("mt", 0, 512, 4), bank("px", 1, 128), F.Copy)
+        act(reg("mt", 512, 1024, 4), reg("px", 512 + 128, 512 + 256), F.Copy)
         act(reg("mt", 1024, 2048, 4), bank("px", 2, 256), F.Copy)
+        d[3] = unpack(3, into[3])
+
+        def project():
+            mm(bank("pu", 2, 128), pair("w", 0, 128), M, ya is None, True, acc=ya)
+            act(reg("ys", t * N * K, (t + 1) * N * K), bank("pu", 2, N * K), F.Copy)
+            dma("y", lambda t=t: T.y[:, t * N * K:(t + 1) * N * K], lambda t=t: T.ys[:, t * N * K:(t + 1) * N * K],
+                r=[reg("ys", t * N * K, (t + 1) * N * K)], sem=out)
+        if t + 1 == R:
+            project()
         red(reg("dv", 0, 1), reg("dm", 0, N * K), A.max)
         ts(reg("fac", 0, NPOW), reg("up", 0, NPOW), reg("dv", 0, 1), A.is_gt, 0.5, A.max)
         scan(reg("hs", 0, NPOW), reg("fac", 0, NPOW), zer(NPOW), -0.25 * 2.0 ** 64)
-        act(reg("gt", 0, 4 * P, 4), bank("px", 3, P), F.Copy, scale=reg("hs", NPOW - 1, NPOW))
-        quant("mt", 0, 256, "mt")
-        d = [mm(bank("px", b, P), pair("e", 128 * b, 128 * b + 128), pair(x, 0, P), True, False) for b in range(4)]
+        ts(reg("gt", 0, 4 * P, 4), reg("gb", 0, P), reg("hs", NPOW - 1, NPOW), A.mult)
+        quant("mt", 0, 128, "mt")
         quant("g", 0, P, "gt")
-        act(reg("ys", t * N * K, (t + 1) * N * K), bank("py", 0, N * K), F.Copy)
+        quant("mt", 128, 128, "mt", 512)
         quant("mt", 256, 256, "mt", 1024)
-        for b in range(4):
-            mm(bank("px", b, P), pair("mt", 128 * b, 128 * b + 128), pair("g", 0, P), False, True, acc=d[b])
-        for b in range(4):
-            if b % 2:
-                cp(reg("rt", b, 4 * P, 4), bank("px", b, P))
-            else:
-                act(reg("rt", b, 4 * P, 4), bank("px", b, P), F.Copy)
+        for b in (1, 0, 3):
+            mm(into[b], slot("mt", b), pair("g", 0, P), b not in d, True, acc=d.get(b))
+        mm(bank("px", 2, 128), slot("mt", 2), pair("g", 0, 128))
+        mm(bank("px", 3, 128), slot("mt", 2), pair("g", P - 128, P))
+        act(reg("rt", 1, 4 * P, 4), into[1], F.Copy)
+        tt(reg("rt", 0, 4 * P, 4), into[0], reg("dx", 0, P), A.add)
+        act(reg("rt", 3, 4 * P, 4), into[3], F.Copy)
+        tt(reg("rt", 2, 512, 4), bank("px", 2, 128), reg("dx", P, P + 128), A.add)
+        tt(reg("rt", 514, 4 * P, 4), reg("px", 1536 + 256 - P, 1536 + 128), reg("dx", P + 128, 2 * P), A.add)
+        if t + 1 < R:
+            project()
         quant(nx, 0, P, "rt")
 
-    last, out = "x%d" % R, T.sem.out
-    for t in range(R):
-        for c, n in ((0, 16), (1, K - 16)):
-            a = reg("plf", 2 * t + c, 2 * t + c + 1, 1, 0, n)
-            dma("y", lambda t=t, c=c, n=n: T.pl[0:1, K * t + 16 * c:K * t + 16 * c + n], lambda a=a: ap(a), r=[a], after=[got], sem=out)
-    dma("y", lambda: T.y[:], lambda: T.ys[:], r=[reg("ys", 0, R * N * K)], sem=out)
+    last = "x%d" % R
     dma("y", lambda: T.oc[:], lambda: T[last + "q"][:].bitcast(dt.uint8), r=[reg(last + "q", 0, P)], sem=out)
     for k in range(4):
         a = reg(last + "s", 0, P, 1, 32 * k, 32 * k + 4)
         dma("s" if k < 2 else "y", lambda k=k: T.osc[4 * k:4 * k + 4, :], lambda a=a: ap(a), r=[a], sem=out)
     emit(ops, queues, T)
-    Y.wait_ge(out, 16 * (2 * R + 6))
+    Y.wait_ge(out, 16 * (3 * R + 5))
     g.wait_ge(T.sem.snd, R * count)

@@ -8,13 +8,13 @@ NPOW = 136
 Q4, U8, BF, F32 = "float8_e4m3fn_x4", "uint8", "bfloat16", "float32"
 
 SCRATCH = {"pu": ("psum", [128, 1536], F32), "px": ("psum", [128, 2048], F32), "pr": ("psum", [128, 512], F32)}
-for _n, _w in (("xt", 4 * P), ("ut", 4), ("wt", 512), ("zer", 512), ("ub", 512), ("kt", 512), ("ct", 4 * P),
+for _n, _w in (("xt", 4 * P), ("ut", 4), ("wt", 512), ("zer", 512), ("ub", 512), ("kt", 512), ("ct", 1024),
                ("dd", P), ("dig", P), ("et", 524), ("mt", 2048), ("gt", 4 * P), ("rt", 4 * P), ("up", NPOW), ("two", NPOW),
                ("fac", NPOW), ("hs", NPOW), ("gb", P)):
     SCRATCH[_n] = ("sbuf", [128, _w], BF)
-for _n, _w in (("ar", P), ("na", 2), ("plf", R), ("fr", 2), ("dm", N * K), ("dv", 1), ("ys", R * N * K), ("dx", 2 * P)):
+for _n, _w in (("ar", P), ("na", 2), ("plf", R), ("pla", 2), ("fr", 2), ("dm", 32), ("dv", 1), ("ys", R * N * K), ("dx", 2 * P)):
     SCRATCH[_n] = ("sbuf", [128, _w], F32)
-for _n, _w in (("u", 128), ("w", 128), ("k0", 128), ("k1", 128), ("c", P), ("e", 512), ("mt", 512), ("g", P),
+for _n, _w in (("u", 128), ("w", 128), ("k0", 128), ("k1", 128), ("c", 256), ("e", 512), ("mt", 512), ("g", P),
                ("x0", P + 128), ("x1", P), ("x2", P), ("l0", 32), ("l1", 224), ("m0", 224), ("m1", 224)):
     SCRATCH[_n + "q"] = ("sbuf", [128, _w], Q4)
     SCRATCH[_n + "s"] = ("sbuf", [128, _w], U8)
@@ -117,9 +117,6 @@ def rank_program(g, core, T, topo):
     def tt(out, in0, in1, o):
         op("v", lambda: V.tensor_tensor(ap(out), ap(in0), ap(in1), o), r=[in0, in1], w=[out])
 
-    def cp(out, in_):
-        op("v", lambda: V.tensor_copy(ap(out), ap(in_)), r=[in_], w=[out])
-
     def red(out, in_, o, neg=False, size=False):
         op("v", lambda: V.tensor_reduce(ap(out), ap(in_), AxisListType.X, o, negate=neg, apply_absolute_value=size),
            r=[in_], w=[out])
@@ -175,15 +172,15 @@ def rank_program(g, core, T, topo):
     zer = lambda n, p0=0, p1=128: reg("zer", 0, n, 1, p0, p1)
     bank = lambda name, b, n, p0=0, p1=128: reg(name, 512 * b, 512 * b + n, 1, p0, p1)
 
+    dma("y", lambda: T.ut[:], lambda: T.u[:], w=[reg("ut", 0, 4)])
     dma("y", lambda: T.xt[:], lambda: T.x[:], w=[reg("xt", 0, 4 * P)])
-    dma("s", lambda: T.ut[:], lambda: T.u[:], w=[reg("ut", 0, 4)])
     fill(zer(512), 0.0)
     fill(reg("et", 0, 524), 0.0)
     iota(reg("dig", 0, P, 1, 0, 64), [[0, P // 16], [1, 16]])
     act(reg("ct", 1, 4 * P, 2), zer(2 * P), F.Identity, 1.0)
     sel(reg("et", 7, 519, 4), zer(128), A.not_equal, 1.0)
     iota(reg("ct", 3, 4 * P, 4, 0, 1), [[16, P // 16], [0, 16]])
-    for a in [reg("gt", 512, 4 * P)] + [reg("mt", 512 * b, 512 * b + 512) for b in range(4)]:
+    for a in [reg("ct", 4 * P, 1024), reg("gt", 512, 4 * P)] + [reg("mt", 512 * b, 512 * b + 512) for b in range(4)]:
         dma("y", lambda a=a: ap(a), lambda a=a: ap(zer(a[2] - a[1])), r=[zer(512)], w=[a])
     dma("y", lambda: T.wt[:], lambda: T.w[:], w=[reg("wt", 0, 512)])
     fill(reg("gt", 1, 512, 2), 0.0)
@@ -224,35 +221,46 @@ def rank_program(g, core, T, topo):
             unpack(0, into[0])
             unpack(2, into[2])
         quant(kk, 0, 128, "kt")
-        act(reg("ar", 0, P), bank("pu", 0, P), F.Abs)
+        act(reg("ar", 0, 64), bank("pu", 0, 64), F.Abs)
+        act(reg("ar", 64, P), reg("pu", 64, P), F.Abs)
         red(naA, bank("pu", 1, 1), A.max, True, True)
         red(naB, bank("pu", 2, 1), A.max, True, True)
-        act(reg("dd", 0, 128), reg("ar", 0, 128), F.Sign, naA)
-        act(reg("dd", 128, P), reg("ar", 128, P), F.Sign, naB)
+        for c0, na in ((0, naA), (64, naA), (128, naB)):
+            act(reg("dd", c0, c0 + 64), reg("ar", c0, c0 + 64), F.Sign, na)
         ts(reg("ct", 512, 4 * P, 4), reg("ar", 128, P), naA, A.add, 0.0, A.is_le)
         ts(reg("ct", 2, 512, 4), reg("ar", 0, 128), naB, A.add, 0.0, A.is_lt)
-        tt(reg("ct", 0, 512, 4), reg("dd", 0, 128), tri(0, 128), A.is_lt)
+        tt(reg("ct", 0, 256, 4), reg("dd", 0, 64), tri(0, 64), A.is_lt)
+        tt(reg("ct", 256, 512, 4), reg("dd", 64, 128), tri(64, 128), A.is_lt)
         tt(reg("ct", 514, 4 * P, 4), reg("dd", 128, P), tri(64, 128), A.is_lt)
         act(reg("dx", 0, P), into[1 - t], F.Copy)
         if t == 1:
             act(reg("dx", P, 2 * P), into[2], F.Copy)
-        quant("c", 0, P, "ct")
-        mm(bank("pu", 1, P), pair(kk, 0, 128), pair("c", 0, P))
-        red(reg("plf", t, t + 1), bank("pu", 1, P), A.min, False, True)
+        for h in range(2):
+            quant("c", 128 * h, 128, "ct", 512 * h)
+        for h in range(2):
+            mm(bank("pu", 1 - h, 128), pair(kk, 0, 128), pair("c", 128 * h, 128 * h + 128))
+        for h in range(2):
+            red(reg("pla", h, h + 1), bank("pu", 1 - h, 128 - 64 * h), A.min, False, True)
         for c in range(2):
             for half in range(2):
-                cp(reg(off[0], c, c + 1, 1, 64 * half, 64 * half + 64), reg("plf", t, t + 1, 1, 64 * c, 64 * c + 64))
+                ts(reg(off[0], c, c + 1, 1, 64 * half, 64 * half + 64), reg("pla", 0, 1, 1, 64 * c, 64 * c + 64),
+                   reg("pla", 1, 2, 1, 64 * c, 64 * c + 64), A.min)
         pick("l%d" % t, LAY * t, 32, x, P, off)
         send(t)
+        ts(reg("plf", t, t + 1), reg("pla", 0, 1), reg("pla", 1, 2), A.min)
 
         if t == 0:
             for b in (2, 1, 3):
                 quant("e", 128 * (b ^ 1), 128, "et", 7 - b)
             fill(reg("two", 0, NPOW), 2.0)
+            fill(reg("dm", 0, 32, 1, N * K, 128), 0.0)
             quant(m, N * K, 128, "zer")
             scan(reg("up", 0, NPOW), reg("two", 0, NPOW), zer(NPOW), 2.0 ** -64)
             quant("w", 0, 128, "wt")
             quant("m1", N * K, 128, "zer")
+            for h in range(2):
+                act(reg("ct", 512 * h + 1, 512 + 256 * h, 4, 64, 65), bank("pu", 1 - h, 128 - 64 * h, 64, 65), F.Relu,
+                    2048.0 * ((K - 16) * GAP - 256.0), -2048.0)
             mm(bank("pu", 0, 128), pair("c", 0, 128), pair(kk, 0, 128))
             mm(bank("pu", 2, 128), pair("c", 64, P), pair(kk, 0, 128))
             unpack(2, into[2])
@@ -265,7 +273,6 @@ def rank_program(g, core, T, topo):
             act(reg("dx", P, 2 * P), into[2], F.Copy)
             for c in range(2):
                 act(reg("kt", 2 * c, 512, 4), reg("kt", 2 * c, 512, 4), F.Relu, scale=reg("fr", c, c + 1))
-            act(reg("ct", 1, 4 * P, 4, 64, 65), bank("pu", 1, P, 64, 65), F.Relu, 2048.0 * ((K - 16) * GAP - 256.0), -2048.0)
             fill(reg("kt", 1, 512, 4, 64, 65), 1.0)
 
         M = pair(m, 0, 128)
@@ -286,7 +293,8 @@ def rank_program(g, core, T, topo):
         for c, n in ((0, 16), (1, K - 16)):
             a = reg("plf", t, t + 1, 1, 64 * c, 64 * c + n)
             dma("y", lambda t=t, c=c, n=n: T.pl[0:1, K * t + 16 * c:K * t + 16 * c + n], lambda a=a: ap(a), r=[a], after=[got], sem=out)
-        tt(reg("dm", 0, N * K), bank("px", 0, N * K), reg("et", 7, 7 + 4 * N * K, 4), A.mult)
+        for a in range(0, N * K, 32):
+            tt(reg("dm", 0, 32, 1, a, a + 32), reg("px", a, a + 32, 1, a, a + 32), reg("et", 7 + 4 * a, 135 + 4 * a, 4, a, a + 32), A.mult)
         act(reg("gb", 0, P), bank("px", 3, P), F.Copy)
         act(reg("mt", 0, 512, 4), bank("px", 1, 128), F.Copy)
         act(reg("mt", 512, 1024, 4), reg("px", 512 + 128, 512 + 256), F.Copy)
@@ -300,7 +308,7 @@ def rank_program(g, core, T, topo):
                 r=[reg("ys", t * N * K, (t + 1) * N * K)], sem=out)
         if t + 1 == R:
             project()
-        red(reg("dv", 0, 1), reg("dm", 0, N * K), A.max)
+        red(reg("dv", 0, 1), reg("dm", 0, 32), A.max)
         ts(reg("fac", 0, NPOW), reg("up", 0, NPOW), reg("dv", 0, 1), A.is_gt, 0.5, A.max)
         scan(reg("hs", 0, NPOW), reg("fac", 0, NPOW), zer(NPOW), -0.25 * 2.0 ** 64)
         ts(reg("gt", 0, 4 * P, 4), reg("gb", 0, P), reg("hs", NPOW - 1, NPOW), A.mult)

@@ -2,24 +2,36 @@ from concourse.bass import DstId, RemoteDMATransfer
 from concourse.mybir import dt, AluOpType, AxisListType, ActivationFunctionType
 
 P, K, R, N = 192, 24, 2, 4
+NK = N * K
 LAY = (N - 1) * K
 GAP = 512.0
 NPOW = 136
+BIG = 2.0 ** 80
 Q4, U8, BF, F32 = "float8_e4m3fn_x4", "uint8", "bfloat16", "float32"
+OPT = {
+    "pre": "zer dig one et sel ktf gtf hi ub3 gt2 kt2 ka kb kc lo ub ktg qu scan qx qe qtri qk",
+    "ch0": "mR mA mB mT aL aH rA rB s0 s1 s2 tA tB t0 t1 t2 q0 q1",
+    "ch1": "mR mA mB qk aL aH rA rB s0 s1 s2 tA tB t0 t1 t2 q0 q1",
+    "df0": "mM mE0 mG mE1 red c0 gb c1 c2 c3 j1 j2 j3a j3b fac scan q0 C q1 qg q2 q3 my cy k0 k1 k2 k3a k3b o0 o1 o2 o3a o3b qA qB",
+    "df1": "mM mE0 mG mE1 red c0 gb c1 c2 c3 j1 j2 j3a j3b fac scan q0 C q1 qg q2 q3 my cy k0 k1 k2 k3a k3b o0 o1 o2 o3a o3b qA qB",
+    "ne": 2, "kept": "1 3a", "bank": {"1": 3, "2": 0, "3a": 2, "3b": 1},
+    "two": False, "halves": False,
+    "split": (False, True),
+}
 
 SCRATCH = {"pu": ("psum", [128, 1536], F32), "px": ("psum", [128, 2048], F32), "pr": ("psum", [128, 512], F32)}
 for _n, _w in (("xt", 4 * P), ("ut", 4), ("wt", 512), ("zer", 512), ("ub", 512), ("kt", 512), ("ct", 1024),
-               ("dd", P), ("dig", P), ("et", 524), ("mt", 2048), ("gt", 4 * P), ("rt", 4 * P), ("up", NPOW), ("two", NPOW),
+               ("dd", P), ("dig", P), ("et", 524), ("mt", 2048), ("gt", 4 * P), ("rt", 1024), ("up", NPOW), ("two", NPOW),
                ("fac", NPOW), ("hs", NPOW), ("gb", P)):
     SCRATCH[_n] = ("sbuf", [128, _w], BF)
-for _n, _w in (("ar", P), ("na", 2), ("plf", R), ("pla", 2), ("fr", 2), ("dm", 32), ("dv", 1), ("ys", R * N * K), ("dx", 2 * P)):
+for _n, _w in (("ar", P), ("na", 2), ("plf", R), ("pla", 2), ("fr", 2), ("dv", 1), ("ys", R * NK), ("dx", 3 * P)):
     SCRATCH[_n] = ("sbuf", [128, _w], F32)
-for _n, _w in (("u", 128), ("w", 128), ("k0", 128), ("k1", 128), ("c", 256), ("e", 512), ("mt", 512), ("g", P),
-               ("x0", P + 128), ("x1", P), ("x2", P), ("l0", 32), ("l1", 224), ("m0", 224), ("m1", 224)):
+for _n, _w in (("u", 128), ("w", 128), ("k0", 128), ("k1", 128), ("c", 256), ("mt", 512), ("g", P),
+               ("x0", 128 + P + 128), ("x1", 256), ("x2", 256), ("l0", 32), ("l1", 224), ("m0", NK + 512), ("m1", 128)):
     SCRATCH[_n + "q"] = ("sbuf", [128, _w], Q4)
     SCRATCH[_n + "s"] = ("sbuf", [128, _w], U8)
 for _t in range(R):
-    SCRATCH["off%d" % _t] = ("sbuf", [128, 2], "uint16")
+    SCRATCH["off%d" % _t] = ("sbuf", [128, 4], "uint16")
 NSEM = 145
 SEMAPHORES = ["arr0", "arr1", "snd", "out"] + ["s%d" % _i for _i in range(NSEM)]
 
@@ -39,10 +51,11 @@ def emit(ops, queues, T):
     for i, o in enumerate(ops):
         deps = set(o["after"])
         o["banks"] = set((a[0], a[1] // 512) for a in o["r"] + o["w"] if SCRATCH[a[0]][0] == "psum")
+        o["names"] = set(a[0] for a in o["r"] + o["w"])
         for j, e in enumerate(ops[:i]):
-            if j != o["acc"] and (any(_meets(a, b) for a in o["w"] for b in e["r"] + e["w"])
-                                  or any(_meets(a, b) for a in o["r"] for b in e["w"])
-                                  or (e["q"] != o["q"] and o["banks"] & e["banks"])):
+            if j not in o["acc"] and not o["names"].isdisjoint(e["names"]) and (any(_meets(a, b) for a in o["w"] for b in e["r"] + e["w"])
+                                      or any(_meets(a, b) for a in o["r"] for b in e["w"])
+                                      or (e["q"] != o["q"] and o["banks"] & e["banks"])):
                 deps.add(j)
         o["waits"], o["done"] = [], {i}
         if o["q"] is not None:
@@ -52,13 +65,20 @@ def emit(ops, queues, T):
                     known[o["q"]] |= ops[j]["done"]
                     ops[j]["by"].append(i)
             o["waits"].sort(key=lambda j: ops[j]["q"] is None)
-            o["done"] = known[o["q"]] | {i} | (ops[o["acc"]]["done"] if o["acc"] is not None else set())
+            o["done"] = (known[o["q"]] | {i}).union(*[ops[j]["done"] for j in o["acc"]])
     teams = {}
     for i, o in enumerate(ops):
         if o["q"] is not None and o["by"]:
             teams.setdefault((o["inc"], tuple(o["by"])), []).append(i)
-    for n, team in enumerate(teams.values()):
-        both = (T.sem["s%d" % n], ops[team[0]]["inc"] * len(team))
+    used = []
+    for team in teams.values():
+        inc = ops[team[0]]["inc"]
+        free = [u for u in used if len(used) == NSEM and u[1] == inc and all(u[2] <= ops[j]["done"] - {j} - set(ops[j]["acc"]) for j in team)]
+        if not free:
+            used.append([len(used), inc, set(), 0])
+        u = free[0] if free else used[-1]
+        u[2], u[3] = u[2] | set(team), u[3] + inc * len(team)
+        both = (T.sem["s%d" % u[0]], u[3])
         for j in team:
             ops[j]["sem"] = both
     for o in ops:
@@ -81,7 +101,7 @@ def rank_program(g, core, T, topo):
     A, F = AluOpType, ActivationFunctionType
     V, S, PE, Y = g.vector, g.scalar, g.tensor, g.sync
     queues = {"g": g, "v": V, "s": S, "t": PE, "y": Y}
-    ops, own = [], []
+    ops, own, outs = [], [], []
 
     def ap(a):
         return T[a[0]][a[4]:a[5], a[1]:a[2]:a[3]] if a[3] != 1 else T[a[0]][a[4]:a[5], a[1]:a[2]]
@@ -92,9 +112,9 @@ def rank_program(g, core, T, topo):
     def val(a):
         return ap(a) if isinstance(a, tuple) else a
 
-    def op(q, fn, r=(), w=(), after=(), acc=None, inc=1, sem=None):
+    def op(q, fn, r=(), w=(), after=(), acc=(), inc=1, sem=None):
         ops.append({"q": q, "fn": fn, "r": [a for a in r if isinstance(a, tuple)], "w": list(w), "after": list(after),
-                    "acc": acc, "inc": inc, "by": [], "sem": sem})
+                    "acc": list(acc), "inc": inc, "by": [], "sem": sem})
         return len(ops) - 1
 
     def pair(name, c0, c1):
@@ -107,7 +127,7 @@ def rank_program(g, core, T, topo):
         (cq, cs), t = pair(name, c0, c0 + n), reg(src, s0, s0 + 4 * n)
         op("v", lambda: V.quantize_mx(ap(cq), ap(cs), ap(t)), r=[t], w=[cq, cs])
 
-    def mm(out, lhs, rhs, start=True, stop=True, acc=None):
+    def mm(out, lhs, rhs, start=True, stop=True, acc=()):
         return op("t", lambda: PE.matmul_mx(ap(out), ap(lhs[0]), ap(lhs[1]), ap(rhs[0]), ap(rhs[1]), start, stop),
                   r=list(lhs) + list(rhs), w=[out], acc=acc)
 
@@ -136,11 +156,20 @@ def rank_program(g, core, T, topo):
     def dma(q, out, in_, r=(), w=(), after=(), sem=None):
         return op(q, lambda: queues[q].dma_start(out(), in_()), r=r, w=w, after=after, inc=16, sem=sem)
 
-    def pick(dst, c0, n, src, width, off):
-        (dq, ds), (sq, ss) = pair(dst, c0, c0 + n), pair(src, 0, width)
+    def store(q, out, a, after=()):
+        outs.append(dma(q, out, lambda: raw(a), r=[a], after=after, sem=T.sem.out))
+
+    def pick(dst, c0, n, src, s0, off):
+        (dq, ds), (sq, ss) = pair(dst, c0, c0 + n), pair(src, s0, s0 + P)
         op("v", lambda: V.tensor_copy(ap(dq).bitcast(dt.uint32), ap(sq).bitcast(dt.uint32).indirect(ap(off))),
            r=[sq, off], w=[dq])
         op("s", lambda: S.activation(ap(ds), ap(ss).indirect(ap(off)), F.Copy), r=[ss, off], w=[ds])
+
+    def play(steps, order):
+        names = order.split()
+        assert sorted(names) == sorted(steps), (sorted(names), sorted(steps))
+        for name in names:
+            steps[name]()
 
     peers = [c for c in T.cores if c != core]
     far = [c for c in peers if topo.chip(c) != topo.chip(core)]
@@ -151,7 +180,7 @@ def rank_program(g, core, T, topo):
     lanes = {c: outer[i * per:(i + 1) * per] for i, c in enumerate(far)}
     spread = inner[::len(inner) // (per * len(near))]
     lanes.update({c: spread[i * per:(i + 1) * per] for i, c in enumerate(near)})
-    count = 2 * per * len(peers)
+    counts = [(1 if OPT["halves"] else 2) * per * len(peers), 2 * per * len(peers)]
 
     def send(t):
         src, dst = pair("l%d" % t, LAY * t, LAY * t + K), pair("m%d" % t, K * rank, K * rank + K)
@@ -160,180 +189,224 @@ def rank_program(g, core, T, topo):
                 trs = []
                 for c in far + near:
                     rid, pid = topo.addr(c)[:2]
-                    trs.append(RemoteDMATransfer(dst_ids=[DstId(rid=rid, pnc=pid)], dma_engine_mask=sum(1 << e for e in lanes[c]),
+                    use = lanes[c][h::2] if t == 0 and OPT["halves"] else lanes[c]
+                    trs.append(RemoteDMATransfer(dst_ids=[DstId(rid=rid, pnc=pid)], dma_engine_mask=sum(1 << e for e in use),
                                                  remote_sem=T.sem["arr%d" % t], src=raw(src[h]), dst=raw(dst[h])))
                 return g.remote_dma_fused(trs, local_sem=T.sem.snd)
             op("g", go, r=[src[h]])
             if t == 0:
                 dma("y", lambda h=h: raw(dst[h]), lambda h=h: raw(src[h]), r=[src[h]], sem=T.sem["arr%d" % t])
         land = [a for c in range(N) if t == 0 or c != rank for a in pair("m%d" % t, K * c, K * c + K)]
-        op(None, None, w=land, sem=(T.sem["arr%d" % t], count + 32 * (1 - t)))
+        op(None, None, w=land, sem=(T.sem["arr%d" % t], counts[t] + 32 * (1 - t)))
 
     zer = lambda n, p0=0, p1=128: reg("zer", 0, n, 1, p0, p1)
     bank = lambda name, b, n, p0=0, p1=128: reg(name, 512 * b, 512 * b + n, 1, p0, p1)
+    E = lambda b, n=128: pair("m0", NK + 128 * b, NK + 128 * b + n)
+    base = [128, 0, 0]
+    X = lambda t, c0, c1: pair("x%d" % t, base[t] + c0, base[t] + c1)
 
     dma("y", lambda: T.ut[:], lambda: T.u[:], w=[reg("ut", 0, 4)])
     dma("y", lambda: T.xt[:], lambda: T.x[:], w=[reg("xt", 0, 4 * P)])
-    fill(zer(512), 0.0)
-    fill(reg("et", 0, 524), 0.0)
-    iota(reg("dig", 0, P, 1, 0, 64), [[0, P // 16], [1, 16]])
-    act(reg("ct", 1, 4 * P, 2), zer(2 * P), F.Identity, 1.0)
-    sel(reg("et", 7, 519, 4), zer(128), A.not_equal, 1.0)
-    iota(reg("ct", 3, 4 * P, 4, 0, 1), [[16, P // 16], [0, 16]])
-    for a in [reg("ct", 4 * P, 1024), reg("gt", 512, 4 * P)] + [reg("mt", 512 * b, 512 * b + 512) for b in range(4)]:
-        dma("y", lambda a=a: ap(a), lambda a=a: ap(zer(a[2] - a[1])), r=[zer(512)], w=[a])
-    dma("y", lambda: T.wt[:], lambda: T.w[:], w=[reg("wt", 0, 512)])
-    fill(reg("gt", 1, 512, 2), 0.0)
-    fill(reg("kt", 1, 512, 2), 0.0)
-    act(reg("gt", 2, 512, 4), zer(128), F.Copy)
-    act(reg("kt", 2, 512, 4, 0, 64), zer(128, 0, 64), F.Copy)
-    fill(reg("kt", 0, 512, 4), GAP)
-    fill(reg("kt", 2, 512, 4, 64, 128), GAP)
-    for b in range(3):
-        ts(reg("ub", b, 512, 4), zer(128), reg("ut", b, b + 1), A.add)
-    act(reg("ub", 3, 512, 4), zer(128), F.Identity, reg("ut", 3, 4))
-    act(reg("kt", 1, 512, 4, 32, 33), reg("dig", 0, 128, 1, 32, 33), F.Copy, scale=-GAP)
-    act(reg("kt", 259, 512, 4, 32, 33), zer(64, 32, 33), F.Identity, -16 * GAP)
-    act(reg("kt", 1, 512, 2, 0, 1), zer(256, 0, 1), F.Identity, 1.0)
-    act(reg("ct", 1, 4 * P, 4, 0, 1), reg("dig", 0, P, 1, 0, 1), F.Copy)
-    scan(reg("gt", 0, 512, 4), zer(128), reg("et", 3, 515, 4), 0.0, A.add)
-    quant("u", 0, 128, "ub")
-    quant("x0", 0, P, "xt")
 
-    naA, naB, out = reg("na", 0, 1), reg("na", 1, 2), T.sem.out
-    tri = lambda c0, c1: reg("pr", P + c0, P + c1)
-    into = [bank("px", 1, P), bank("pr", 0, P), bank("px", 2, P), bank("px", 0, P)]
-    slot = lambda name, b: pair(name, 128 * (b ^ 1), 128 * (b ^ 1) + 128)
+    def et():
+        fill(reg("et", 0, 524), 0.0)
+
+    def zeros():
+        fill(zer(512), 0.0)
+        for a in [reg("ct", 4 * P, 1024), reg("gt", 512, 4 * P)] + [reg("mt", 512 * b, 512 * b + 512) for b in range(4)] + [reg("rt", 4 * P, 1024)]:
+            dma("y", lambda a=a: ap(a), lambda a=a: ap(zer(a[2] - a[1])), r=[zer(512)], w=[a])
+
+    def ub():
+        for b in range(3):
+            ts(reg("ub", b, 512, 4), zer(128), reg("ut", b, b + 1), A.add)
+
+    def ktg():
+        fill(reg("kt", 0, 512, 4), GAP)
+        fill(reg("kt", 2, 512, 4, 64, 128), GAP)
+    play({"sel": lambda: sel(reg("et", 7, 519, 4), reg("et", 7, 519, 4), A.not_equal, 1.0),
+          "dig": lambda: iota(reg("dig", 0, P, 1, 0, 64), [[0, P // 16], [1, 16]]),
+          "hi": lambda: iota(reg("ct", 3, 4 * P, 4, 0, 1), [[16, P // 16], [0, 16]]),
+          "gt2": lambda: act(reg("gt", 2, 512, 4), zer(128), F.Copy),
+          "one": lambda: act(reg("ct", 1, 4 * P, 2), zer(2 * P), F.Identity, 1.0),
+          "kt2": lambda: act(reg("kt", 2, 512, 4, 0, 64), zer(128, 0, 64), F.Copy),
+          "ub3": lambda: act(reg("ub", 3, 512, 4), zer(128), F.Identity, reg("ut", 3, 4)),
+          "ka": lambda: act(reg("kt", 1, 512, 4, 32, 33), reg("dig", 0, 128, 1, 32, 33), F.Copy, scale=-GAP),
+          "kb": lambda: act(reg("kt", 259, 512, 4, 32, 33), zer(64, 32, 33), F.Identity, -16 * GAP),
+          "kc": lambda: act(reg("kt", 1, 512, 2, 0, 1), zer(256, 0, 1), F.Identity, 1.0),
+          "lo": lambda: act(reg("ct", 1, 4 * P, 4, 0, 1), reg("dig", 0, P, 1, 0, 1), F.Copy),
+          "et": et, "zer": zeros, "gtf": lambda: fill(reg("gt", 1, 512, 2), 0.0), "ktf": lambda: fill(reg("kt", 1, 512, 2), 0.0),
+          "scan": lambda: scan(reg("gt", 0, 512, 4), zer(128), reg("et", 3, 515, 4), 0.0, A.add),
+          "qe": lambda: quant("m0", NK, 128, "et", 7), "ub": ub, "qtri": lambda: quant("x0", base[0] + P, 128, "gt"),
+          "qu": lambda: quant("u", 0, 128, "ub"), "qx": lambda: quant("x0", base[0], P, "xt"), "ktg": ktg,
+          "qk": lambda: quant("k0", 0, 128, "kt")}, OPT["pre"])
+
+    naA, naB = reg("na", 0, 1), reg("na", 1, 2)
+    parts = {"0": (0, 0, P, 0), "1": (1, 0, P, 0), "2": (2, 0, P, 0), "3a": (3, 0, 128, 0), "3b": (3, 64, P, 128)}
+    home = {name: ("pr", 0) if name == "0" else ("px", 512 * OPT["bank"][name]) for name in parts}
+    wide = lambda name: reg(home[name][0], home[name][1], home[name][1] + parts[name][2] - parts[name][1])
+    used = lambda name: reg(home[name][0], home[name][1] + parts[name][3] - parts[name][1], home[name][1] + parts[name][2] - parts[name][1])
+    held = lambda name: reg("dx", P * (parts[name][0] - 1) + parts[name][3], P * (parts[name][0] - 1) + parts[name][2])
+    kept = OPT["kept"].split()
+    into = [bank("pr", 0, P)]
     for t in range(R):
-        x, nx, kk, m = "x%d" % t, "x%d" % (t + 1), "k%d" % t, "m%d" % t
-        off = reg("off%d" % t, 0, 2)
-        unpack = lambda b, to, n=P: mm(to, slot("e", b), pair(x, 0, n), True, b % 2 == 0)
+        kk, m = "k%d" % t, "m%d" % t
+        tri = (lambda c0, c1: reg("px", 1536 + 2 + c0, 1536 + 2 + c1)) if t == 0 else (lambda c0, c1: reg("pr", P + c0, P + c1))
         d = {}
-        mm(bank("pu", 0, P), pair("u", 0, 128), pair(x, 0, P))
-        mm(bank("pu", 1, 128), pair(x, 0, 128), pair("u", 0, 128))
-        mm(bank("pu", 2, 128), pair(x, 64, P), pair("u", 0, 128))
+
+        def aside():
+            for name in kept:
+                mm(wide(name), E(parts[name][0]), X(t, parts[name][1], parts[name][2]))
+            for name in kept:
+                act(held(name), used(name), F.Copy)
+
+        steps = {
+            "mR": lambda: mm(bank("pu", 0, P), pair("u", 0, 128), X(t, 0, P)),
+            "mA": lambda: mm(bank("pu", 1, 128), X(t, 0, 128), pair("u", 0, 128)),
+            "mB": lambda: mm(bank("pu", 2, 128), X(t, 64, P), pair("u", 0, 128)),
+            "aL": lambda: act(reg("ar", 0, 64), bank("pu", 0, 64), F.Abs),
+            "aH": lambda: act(reg("ar", 64, P), reg("pu", 64, P), F.Abs),
+            "rA": lambda: red(naA, bank("pu", 1, 1), A.max, True, True),
+            "rB": lambda: red(naB, bank("pu", 2, 1), A.max, True, True),
+            "s0": lambda: act(reg("dd", 0, 64), reg("ar", 0, 64), F.Sign, naA),
+            "s1": lambda: act(reg("dd", 64, 128), reg("ar", 64, 128), F.Sign, naA),
+            "s2": lambda: act(reg("dd", 128, P), reg("ar", 128, P), F.Sign, naB),
+            "tA": lambda: ts(reg("ct", 512, 4 * P, 4), reg("ar", 128, P), naA, A.add, 0.0, A.is_le),
+            "tB": lambda: ts(reg("ct", 2, 512, 4), reg("ar", 0, 128), naB, A.add, 0.0, A.is_lt),
+            "t0": lambda: tt(reg("ct", 0, 256, 4), reg("dd", 0, 64), tri(0, 64), A.is_lt),
+            "t1": lambda: tt(reg("ct", 256, 512, 4), reg("dd", 64, 128), tri(64, 128), A.is_lt),
+            "t2": lambda: tt(reg("ct", 514, 4 * P, 4), reg("dd", 128, P), tri(64, 128), A.is_lt),
+            "q0": lambda: quant("c", 0, 128, "ct", 0),
+            "q1": lambda: quant("c", 128, 128, "ct", 512),
+        }
         if t == 0:
-            quant("e", 128, 128, "et", 7)
-            quant(x, P, 128, "gt")
-            unpack(0, bank("pr", 0, P + 128), P + 128)
+            steps["mT"] = lambda: mm(bank("px", 3, 130), E(0), X(0, P - 2, P + 128))
         else:
-            quant("l1", 0, 128, "zer")
-            unpack(0, into[0])
-            unpack(2, into[2])
-        quant(kk, 0, 128, "kt")
-        act(reg("ar", 0, 64), bank("pu", 0, 64), F.Abs)
-        act(reg("ar", 64, P), reg("pu", 64, P), F.Abs)
-        red(naA, bank("pu", 1, 1), A.max, True, True)
-        red(naB, bank("pu", 2, 1), A.max, True, True)
-        for c0, na in ((0, naA), (64, naA), (128, naB)):
-            act(reg("dd", c0, c0 + 64), reg("ar", c0, c0 + 64), F.Sign, na)
-        ts(reg("ct", 512, 4 * P, 4), reg("ar", 128, P), naA, A.add, 0.0, A.is_le)
-        ts(reg("ct", 2, 512, 4), reg("ar", 0, 128), naB, A.add, 0.0, A.is_lt)
-        tt(reg("ct", 0, 256, 4), reg("dd", 0, 64), tri(0, 64), A.is_lt)
-        tt(reg("ct", 256, 512, 4), reg("dd", 64, 128), tri(64, 128), A.is_lt)
-        tt(reg("ct", 514, 4 * P, 4), reg("dd", 128, P), tri(64, 128), A.is_lt)
-        act(reg("dx", 0, P), into[1 - t], F.Copy)
+            steps["qk"] = lambda: quant(kk, 0, 128, "kt")
+        play(steps, OPT["ch%d" % t])
         if t == 1:
-            act(reg("dx", P, 2 * P), into[2], F.Copy)
-        for h in range(2):
-            quant("c", 128 * h, 128, "ct", 512 * h)
+            aside()
+            quant("w", 0, 128, "wt")
+        else:
+            act(reg("mt", 128, 512, 4, 0, NK), reg("et", 7, 7 + 4 * NK, 4, 0, NK), F.Identity, -BIG, BIG)
+            quant("x0", 0, 128, "mt")
+            act(reg("two", 0, NPOW), zer(NPOW), F.Identity, 2.0)
+            act(reg("gt", 0, 512, 4, NK, 128), zer(128, NK, 128), F.Copy)
+            act(reg("kt", 1, 512, 4, 64, 65), zer(128, 64, 65), F.Identity, 1.0)
         for h in range(2):
             mm(bank("pu", 1 - h, 128), pair(kk, 0, 128), pair("c", 128 * h, 128 * h + 128))
         for h in range(2):
             red(reg("pla", h, h + 1), bank("pu", 1 - h, 128 - 64 * h), A.min, False, True)
+        gap = 2 if OPT["two"] else 1
         for c in range(2):
             for half in range(2):
-                ts(reg(off[0], c, c + 1, 1, 64 * half, 64 * half + 64), reg("pla", 0, 1, 1, 64 * c, 64 * c + 64),
+                ts(reg("off%d" % t, gap * c, gap * c + 1, 1, 64 * half, 64 * half + 64), reg("pla", 0, 1, 1, 64 * c, 64 * c + 64),
                    reg("pla", 1, 2, 1, 64 * c, 64 * c + 64), A.min)
-        pick("l%d" % t, LAY * t, 32, x, P, off)
+        if OPT["two"]:
+            for c in range(2):
+                pick("l%d" % t, LAY * t + 16 * c, 16, "x%d" % t, base[t], reg("off%d" % t, 2 * c, 2 * c + 1))
+        else:
+            pick("l%d" % t, LAY * t, 32, "x%d" % t, base[t], reg("off%d" % t, 0, 2))
         send(t)
         ts(reg("plf", t, t + 1), reg("pla", 0, 1), reg("pla", 1, 2), A.min)
 
         if t == 0:
-            for b in (2, 1, 3):
-                quant("e", 128 * (b ^ 1), 128, "et", 7 - b)
-            fill(reg("two", 0, NPOW), 2.0)
-            fill(reg("dm", 0, 32, 1, N * K, 128), 0.0)
-            quant(m, N * K, 128, "zer")
+            for b in (2, 3, 1):
+                quant("m0", NK + 128 * b, 128, "et", 7 - b)
             scan(reg("up", 0, NPOW), reg("two", 0, NPOW), zer(NPOW), 2.0 ** -64)
-            quant("w", 0, 128, "wt")
-            quant("m1", N * K, 128, "zer")
             for h in range(2):
                 act(reg("ct", 512 * h + 1, 512 + 256 * h, 4, 64, 65), bank("pu", 1 - h, 128 - 64 * h, 64, 65), F.Relu,
                     2048.0 * ((K - 16) * GAP - 256.0), -2048.0)
+            d["0"] = mm(bank("pr", 0, P + 128), E(0), X(0, 0, P + 128), True, False)
+        else:
+            quant("l1", NK, 128, "zer")
+            d["0"] = mm(into[0], E(0), X(t, 0, P), True, False)
+        mask = mm(bank("px", 0, 128), E(0), pair("x0", base[0] - NK, base[0] - NK + 128), True, False)
+        if t == 0:
+            quant("l1", 0, 128, "zer")
+            aside()
             mm(bank("pu", 0, 128), pair("c", 0, 128), pair(kk, 0, 128))
             mm(bank("pu", 2, 128), pair("c", 64, P), pair(kk, 0, 128))
-            unpack(2, into[2])
-        else:
-            quant("l1", N * K, 128, "zer")
-        d[1] = unpack(1, into[1])
-        if t == 0:
             act(reg("fr", 0, 1), bank("pu", 0, 1), F.Sign, 256.0 - K * GAP)
             act(reg("fr", 1, 2), bank("pu", 2, 1), F.Sign, 256.0 - K * GAP)
-            act(reg("dx", P, 2 * P), into[2], F.Copy)
+        else:
+            mm(bank("pu", 1, 128), pair("w", 0, 128), pair("m0", 0, 128))
+            act(reg("ys", 0, NK), bank("pu", 1, NK), F.Copy)
+
+        def weights():
             for c in range(2):
                 act(reg("kt", 2 * c, 512, 4), reg("kt", 2 * c, 512, 4), F.Relu, scale=reg("fr", c, c + 1))
-            fill(reg("kt", 1, 512, 4, 64, 65), 1.0)
 
         M = pair(m, 0, 128)
-
-        def with_m(a, start, stop, acc):
-            return [mm(bank("px", 0, 128), a, a, start, stop, acc[0]), mm(bank("px", 3, P), a, pair(x, 0, P), start, stop, acc[1]),
-                    mm(bank("px", 1, 256), a, pair("e", 0, 256), start, stop, acc[2]),
-                    mm(bank("px", 2, 256), a, pair("e", 256, 512), start, stop, acc[3])]
-        if t == 0:
-            ya, got = None, with_m(M, True, True, [None] * 4)[0]
-            for a, b in zip(pair("m1", K * rank, K * rank + K), pair("m1", N * K, N * K + K)):
-                dma("y", lambda a=a: raw(a), lambda b=b: raw(b), r=[b], w=[a], after=[got])
-        else:
+        ne = OPT["ne"]
+        outb = [bank("px", 0, 128), bank("px", 3, P), bank("px", 1, 128 * ne), bank("px", 2, 512 - 128 * ne)]
+        side = lambda a: [a, X(t, 0, P), E(0, 128 * ne), E(ne, 512 - 128 * ne)]
+        early, ya = [[mask], [], [], []], []
+        if t == 1:
             mine = pair("l1", LAY - K * rank, LAY - K * rank + 128)
-            early = with_m(mine, True, False, [None] * 4)
-            ya = mm(bank("pu", 2, 128), pair("w", 0, 128), mine, True, False)
-            got = with_m(M, False, True, early)[0]
-        for c, n in ((0, 16), (1, K - 16)):
-            a = reg("plf", t, t + 1, 1, 64 * c, 64 * c + n)
-            dma("y", lambda t=t, c=c, n=n: T.pl[0:1, K * t + 16 * c:K * t + 16 * c + n], lambda a=a: ap(a), r=[a], after=[got], sem=out)
-        for a in range(0, N * K, 32):
-            tt(reg("dm", 0, 32, 1, a, a + 32), reg("px", a, a + 32, 1, a, a + 32), reg("et", 7 + 4 * a, 135 + 4 * a, 4, a, a + 32), A.mult)
-        act(reg("gb", 0, P), bank("px", 3, P), F.Copy)
-        act(reg("mt", 0, 512, 4), bank("px", 1, 128), F.Copy)
-        act(reg("mt", 512, 1024, 4), reg("px", 512 + 128, 512 + 256), F.Copy)
-        act(reg("mt", 1024, 2048, 4), bank("px", 2, 256), F.Copy)
-        d[3] = unpack(3, into[3])
+            for i in range(4):
+                early[i].append(mm(outb[i], mine, side(mine)[i], i > 0, False, early[i]))
+            ya.append(mm(bank("pu", 2, 128), pair("w", 0, 128), mine, True, False))
+        with_m = lambda i: mm(outb[i], M, side(M)[i], not early[i], True, early[i])
 
-        def project():
-            mm(bank("pu", 2, 128), pair("w", 0, 128), M, ya is None, True, acc=ya)
-            act(reg("ys", t * N * K, (t + 1) * N * K), bank("pu", 2, N * K), F.Copy)
-            dma("y", lambda t=t: T.y[:, t * N * K:(t + 1) * N * K], lambda t=t: T.ys[:, t * N * K:(t + 1) * N * K],
-                r=[reg("ys", t * N * K, (t + 1) * N * K)], sem=out)
-        if t + 1 == R:
-            project()
-        red(reg("dv", 0, 1), reg("dm", 0, 32), A.max)
-        ts(reg("fac", 0, NPOW), reg("up", 0, NPOW), reg("dv", 0, 1), A.is_gt, 0.5, A.max)
-        scan(reg("hs", 0, NPOW), reg("fac", 0, NPOW), zer(NPOW), -0.25 * 2.0 ** 64)
-        ts(reg("gt", 0, 4 * P, 4), reg("gb", 0, P), reg("hs", NPOW - 1, NPOW), A.mult)
-        quant("mt", 0, 128, "mt")
-        quant("g", 0, P, "gt")
-        quant("mt", 128, 128, "mt", 512)
-        quant("mt", 256, 256, "mt", 1024)
-        for b in (1, 0, 3):
-            mm(into[b], slot("mt", b), pair("g", 0, P), b not in d, True, acc=d.get(b))
-        mm(bank("px", 2, 128), slot("mt", 2), pair("g", 0, 128))
-        mm(bank("px", 3, 128), slot("mt", 2), pair("g", P - 128, P))
-        act(reg("rt", 1, 4 * P, 4), into[1], F.Copy)
-        tt(reg("rt", 0, 4 * P, 4), into[0], reg("dx", 0, P), A.add)
-        act(reg("rt", 3, 4 * P, 4), into[3], F.Copy)
-        tt(reg("rt", 2, 512, 4), bank("px", 2, 128), reg("dx", P, P + 128), A.add)
-        tt(reg("rt", 514, 4 * P, 4), reg("px", 1536 + 256 - P, 1536 + 128), reg("dx", P + 128, 2 * P), A.add)
-        if t + 1 < R:
-            project()
-        quant(nx, 0, P, "rt")
+        def first():
+            got = with_m(0)
+            if t == 0:
+                for a, b in zip(pair("m1", K * rank, K * rank + K) + pair("m1", NK, 128), pair("l1", 0, K) + pair("l1", 0, 32)):
+                    dma("y", lambda a=a: raw(a), lambda b=b: raw(b), r=[b], w=[a], after=[got])
+                dma("y", lambda: T.wt[:], lambda: T.w[:], w=[reg("wt", 0, 512)], after=[got])
+            else:
+                store("y", lambda: T.y[:, 0:NK], reg("ys", 0, NK), [got])
+            for c, n in ((0, 16), (1, K - 16)):
+                store("y", lambda t=t, c=c, n=n: T.pl[0:1, K * t + 16 * c:K * t + 16 * c + n], reg("plf", t, t + 1, 1, 64 * c, 64 * c + n), [got])
 
-    last = "x%d" % R
-    dma("y", lambda: T.oc[:], lambda: T[last + "q"][:].bitcast(dt.uint8), r=[reg(last + "q", 0, P)], sem=out)
+        def again(name):
+            if name not in kept:
+                d[name] = mm(wide(name), E(parts[name][0]), X(t, parts[name][1], parts[name][2]), True, False)
+
+        def fix(name):
+            b, acc = parts[name][0], [d[name]] if name in d else []
+            mm(wide(name), pair("mt", 128 * b, 128 * b + 128), pair("g", parts[name][1], parts[name][2]), not acc, True, acc)
+
+        def done(name):
+            b, c0, c1 = parts[name][0], parts[name][3], parts[name][2]
+            if name in kept:
+                tt(reg("rt", 4 * c0 + b, 4 * c1, 4), used(name), held(name), A.add)
+            else:
+                act(reg("rt", 4 * c0 + b, 4 * c1, 4), used(name), F.Copy)
+
+        def out_y():
+            act(reg("ys", NK, 2 * NK), bank("pu", 2, NK), F.Copy)
+            store("y", lambda: T.y[:, NK:2 * NK], reg("ys", NK, 2 * NK))
+
+        def table(c0, n):
+            quant("x%d" % (t + 1), c0, n, "rt", 4 * c0)
+            if t + 1 == R:
+                c1 = min(c0 + n, P)
+                store("y", lambda: T.oc[:, 4 * c0:4 * c1], reg("x%dq" % R, c0, c1))
+        at = lambda b: 512 + 128 * b if b < ne else 1024 + 128 * (b - ne)
+        turned = lambda b: act(reg("mt", 512 * b, 512 * b + 512, 4, 0, NK), reg("px", at(b), at(b) + 128, 1, 0, NK), F.Copy)
+        rows = lambda name, c0, c1, step=1: reg(name, c0, c1, step, 0, NK)
+        none = lambda: None
+        play({
+            "mM": first, "mG": lambda: with_m(1), "mE0": lambda: with_m(2), "mE1": lambda: with_m(3),
+            "red": lambda: red(rows("dv", 0, 1), rows("px", 0, NK), A.max),
+            "gb": lambda: act(rows("gb", 0, P), rows("px", 1536, 1536 + P), F.Copy),
+            "c0": lambda: turned(0), "c1": lambda: turned(1), "c2": lambda: turned(2), "c3": lambda: turned(3),
+            "fac": lambda: ts(rows("fac", 0, NPOW), rows("up", 0, NPOW), rows("dv", 0, 1), A.is_gt, 0.5, A.max),
+            "scan": lambda: scan(rows("hs", 0, NPOW), rows("fac", 0, NPOW), zer(NPOW, 0, NK), -0.25 * 2.0 ** 64),
+            "C": lambda: ts(rows("gt", 0, 4 * P, 4), rows("gb", 0, P), rows("hs", NPOW - 1, NPOW), A.mult),
+            "qg": lambda: quant("g", 0, P, "gt"),
+            "q0": lambda: quant("mt", 0, 128, "mt", 0), "q1": lambda: quant("mt", 128, 128, "mt", 512),
+            "q2": lambda: quant("mt", 256, 128, "mt", 1024), "q3": lambda: quant("mt", 384, 128, "mt", 1536),
+            "my": (lambda: mm(bank("pu", 2, 128), pair("w", 0, 128), M, False, True, ya)) if t == 1 else none,
+            "cy": out_y if t == 1 else weights,
+            **{"k" + name: (lambda name=name: fix(name)) for name in parts}, **{"o" + name: (lambda name=name: done(name)) for name in parts},
+            **{"j" + name: (lambda name=name: again(name)) for name in parts if name != "0"},
+            "qA": lambda: table(0, 128) if OPT["split"][t] else None, "qB": lambda: table(128, 128) if OPT["split"][t] else table(0, P),
+        }, OPT["df%d" % t])
+
     for k in range(4):
-        a = reg(last + "s", 0, P, 1, 32 * k, 32 * k + 4)
-        dma("s" if k < 2 else "y", lambda k=k: T.osc[4 * k:4 * k + 4, :], lambda a=a: ap(a), r=[a], sem=out)
+        store("s" if k < 3 else "y", lambda k=k: T.osc[4 * k:4 * k + 4, :], reg("x%ds" % R, 0, P, 1, 32 * k, 32 * k + 4))
     emit(ops, queues, T)
-    Y.wait_ge(out, 16 * (3 * R + 5))
-    g.wait_ge(T.sem.snd, R * count)
+    Y.wait_ge(T.sem.out, 16 * len(outs))
+    g.wait_ge(T.sem.snd, sum(counts))

from concourse.bass import DstId, RemoteDMATransfer
from concourse.mybir import dt, AluOpType, AxisListType, ActivationFunctionType

P, K, R, N = 192, 24, 2, 4
NK = N * K
LAY = (N - 1) * K
GAP = 512.0
NPOW = 136
BIG = 2.0 ** 80
Q4, U8, BF, F32 = "float8_e4m3fn_x4", "uint8", "bfloat16", "float32"
OPT = {
    "pre": "zer dig one et sel ktf gtf hi ub3 gt2 kt2 ka kb kc lo ub ktg qu scan qx qe qtri qk",
    "ch0": "mR mA mB mT aL aH rA rB s0 s1 s2 tA tB t0 t1 t2 q0 q1",
    "ch1": "mR mA mB qk aL aH rA rB s0 s1 s2 tA tB t0 t1 t2 q0 q1",
    "df0": "mM mE0 mG mE1 red c0 gb c1 c2 c3 j1 j2 j3a j3b fac scan q0 C q1 qg q2 q3 my cy k0 k1 k2 k3a k3b o0 o1 o2 o3a o3b qA qB",
    "df1": "mM mE0 mG mE1 red c0 gb c1 c2 c3 j1 j2 j3a j3b fac scan q0 C q1 qg q2 q3 my cy k0 k1 k2 k3a k3b o0 o1 o2 o3a o3b qA qB",
    "ne": 2, "kept": "1 3a", "bank": {"1": 3, "2": 0, "3a": 2, "3b": 1},
    "two": False, "halves": False,
    "split": (False, True),
}

SCRATCH = {"pu": ("psum", [128, 1536], F32), "px": ("psum", [128, 2048], F32), "pr": ("psum", [128, 512], F32)}
for _n, _w in (("xt", 4 * P), ("ut", 4), ("wt", 512), ("zer", 512), ("ub", 512), ("kt", 512), ("ct", 1024),
               ("dd", P), ("dig", P), ("et", 524), ("mt", 2048), ("gt", 4 * P), ("rt", 1024), ("up", NPOW), ("two", NPOW),
               ("fac", NPOW), ("hs", NPOW), ("gb", P)):
    SCRATCH[_n] = ("sbuf", [128, _w], BF)
for _n, _w in (("ar", P), ("na", 2), ("plf", R), ("pla", 2), ("fr", 2), ("dv", 1), ("ys", R * NK), ("dx", 3 * P)):
    SCRATCH[_n] = ("sbuf", [128, _w], F32)
for _n, _w in (("u", 128), ("w", 128), ("k0", 128), ("k1", 128), ("c", 256), ("mt", 512), ("g", P),
               ("x0", 128 + P + 128), ("x1", 256), ("x2", 256), ("l0", 32), ("l1", 224), ("m0", NK + 512), ("m1", 128)):
    SCRATCH[_n + "q"] = ("sbuf", [128, _w], Q4)
    SCRATCH[_n + "s"] = ("sbuf", [128, _w], U8)
for _t in range(R):
    SCRATCH["off%d" % _t] = ("sbuf", [128, 4], "uint16")
NSEM = 145
SEMAPHORES = ["arr0", "arr1", "snd", "out"] + ["s%d" % _i for _i in range(NSEM)]


def reg(name, c0, c1, step=1, p0=0, p1=128):
    return (name, c0, c1, step, p0, p1)


def _meets(a, b):
    if a[0] != b[0] or a[5] <= b[4] or b[5] <= a[4]:
        return False
    return not set(range(a[1], a[2], a[3])).isdisjoint(range(b[1], b[2], b[3]))


def emit(ops, queues, T):
    known = {q: set() for q in queues}
    for i, o in enumerate(ops):
        deps = set(o["after"])
        o["banks"] = set((a[0], a[1] // 512) for a in o["r"] + o["w"] if SCRATCH[a[0]][0] == "psum")
        o["names"] = set(a[0] for a in o["r"] + o["w"])
        for j, e in enumerate(ops[:i]):
            if j not in o["acc"] and not o["names"].isdisjoint(e["names"]) and (any(_meets(a, b) for a in o["w"] for b in e["r"] + e["w"])
                                      or any(_meets(a, b) for a in o["r"] for b in e["w"])
                                      or (e["q"] != o["q"] and o["banks"] & e["banks"])):
                deps.add(j)
        o["waits"], o["done"] = [], {i}
        if o["q"] is not None:
            for j in sorted(deps, reverse=True):
                if j not in known[o["q"]]:
                    o["waits"].insert(0, j)
                    known[o["q"]] |= ops[j]["done"]
                    ops[j]["by"].append(i)
            o["waits"].sort(key=lambda j: ops[j]["q"] is None)
            o["done"] = (known[o["q"]] | {i}).union(*[ops[j]["done"] for j in o["acc"]])
    teams = {}
    for i, o in enumerate(ops):
        if o["q"] is not None and o["by"]:
            teams.setdefault((o["inc"], tuple(o["by"])), []).append(i)
    used = []
    for team in teams.values():
        inc = ops[team[0]]["inc"]
        free = [u for u in used if len(used) == NSEM and u[1] == inc and all(u[2] <= ops[j]["done"] - {j} - set(ops[j]["acc"]) for j in team)]
        if not free:
            used.append([len(used), inc, set(), 0])
        u = free[0] if free else used[-1]
        u[2], u[3] = u[2] | set(team), u[3] + inc * len(team)
        both = (T.sem["s%d" % u[0]], u[3])
        for j in team:
            ops[j]["sem"] = both
    for o in ops:
        if o["q"] is None:
            continue
        seen = []
        for j in o["waits"]:
            if not any(ops[j]["sem"] is s for s in seen):
                seen.append(ops[j]["sem"])
                queues[o["q"]].wait_ge(*ops[j]["sem"])
        ins = o["fn"]()
        if o["sem"] is not None:
            ins.then_inc(o["sem"][0] if o["by"] else o["sem"], o["inc"])


def rank_program(g, core, T, topo):
    rank = T.rank_of(core)
    if rank is None:
        return
    A, F = AluOpType, ActivationFunctionType
    V, S, PE, Y = g.vector, g.scalar, g.tensor, g.sync
    queues = {"g": g, "v": V, "s": S, "t": PE, "y": Y}
    ops, own, outs = [], [], []

    def ap(a):
        return T[a[0]][a[4]:a[5], a[1]:a[2]:a[3]] if a[3] != 1 else T[a[0]][a[4]:a[5], a[1]:a[2]]

    def raw(a):
        return ap(a).bitcast(dt.uint8) if SCRATCH[a[0]][2] == Q4 else ap(a)

    def val(a):
        return ap(a) if isinstance(a, tuple) else a

    def op(q, fn, r=(), w=(), after=(), acc=(), inc=1, sem=None):
        ops.append({"q": q, "fn": fn, "r": [a for a in r if isinstance(a, tuple)], "w": list(w), "after": list(after),
                    "acc": list(acc), "inc": inc, "by": [], "sem": sem})
        return len(ops) - 1

    def pair(name, c0, c1):
        return reg(name + "q", c0, c1), reg(name + "s", c0, c1)

    def fill(out, c):
        op("v", lambda: V.memset(ap(out), c), w=[out])

    def quant(name, c0, n, src, s0=0):
        (cq, cs), t = pair(name, c0, c0 + n), reg(src, s0, s0 + 4 * n)
        op("v", lambda: V.quantize_mx(ap(cq), ap(cs), ap(t)), r=[t], w=[cq, cs])

    def mm(out, lhs, rhs, start=True, stop=True, acc=()):
        return op("t", lambda: PE.matmul_mx(ap(out), ap(lhs[0]), ap(lhs[1]), ap(rhs[0]), ap(rhs[1]), start, stop),
                  r=list(lhs) + list(rhs), w=[out], acc=acc)

    def ts(out, in0, s1, op0, s2=None, *op1):
        op("v", lambda: V.tensor_scalar(ap(out), ap(in0), val(s1), s2, op0, *op1), r=[in0, s1], w=[out])

    def tt(out, in0, in1, o):
        op("v", lambda: V.tensor_tensor(ap(out), ap(in0), ap(in1), o), r=[in0, in1], w=[out])

    def red(out, in_, o, neg=False, size=False):
        op("v", lambda: V.tensor_reduce(ap(out), ap(in_), AxisListType.X, o, negate=neg, apply_absolute_value=size),
           r=[in_], w=[out])

    def scan(out, d0, d1, first, o=A.mult):
        op("v", lambda: V.tensor_tensor_scan(ap(out), ap(d0), ap(d1), first, o, A.add), r=[d0, d1], w=[out])

    def act(out, in_, f, bias=0.0, scale=1.0):
        op("s", lambda: S.activation(ap(out), ap(in_), f, bias=val(bias), scale=val(scale)), r=[in_, bias, scale], w=[out])

    def iota(out, pattern):
        own.append(op("g", lambda: g.iota(ap(out), pattern, 0, 0, allow_small_or_imprecise_dtypes=True), w=[out], after=own[-1:]))

    def sel(out, in_, cmp, c):
        own.append(op("g", lambda: g.affine_select(ap(out), ap(in_), [[-1, 128]], cmp, c, 0, 1), r=[in_], w=[out], after=own[-1:]))

    def dma(q, out, in_, r=(), w=(), after=(), sem=None):
        return op(q, lambda: queues[q].dma_start(out(), in_()), r=r, w=w, after=after, inc=16, sem=sem)

    def store(q, out, a, after=()):
        outs.append(dma(q, out, lambda: raw(a), r=[a], after=after, sem=T.sem.out))

    def pick(dst, c0, n, src, s0, off):
        (dq, ds), (sq, ss) = pair(dst, c0, c0 + n), pair(src, s0, s0 + P)
        op("v", lambda: V.tensor_copy(ap(dq).bitcast(dt.uint32), ap(sq).bitcast(dt.uint32).indirect(ap(off))),
           r=[sq, off], w=[dq])
        op("s", lambda: S.activation(ap(ds), ap(ss).indirect(ap(off)), F.Copy), r=[ss, off], w=[ds])

    def play(steps, order):
        names = order.split()
        assert sorted(names) == sorted(steps), (sorted(names), sorted(steps))
        for name in names:
            steps[name]()

    peers = [c for c in T.cores if c != core]
    far = [c for c in peers if topo.chip(c) != topo.chip(core)]
    near = [c for c in peers if topo.chip(c) == topo.chip(core)]
    outer = topo.engines(core, far[0])
    inner = [e for e in topo.engines(core, near[0]) if e not in outer]
    per = len(outer) // len(far)
    lanes = {c: outer[i * per:(i + 1) * per] for i, c in enumerate(far)}
    spread = inner[::len(inner) // (per * len(near))]
    lanes.update({c: spread[i * per:(i + 1) * per] for i, c in enumerate(near)})
    counts = [(1 if OPT["halves"] else 2) * per * len(peers), 2 * per * len(peers)]

    def send(t):
        src, dst = pair("l%d" % t, LAY * t, LAY * t + K), pair("m%d" % t, K * rank, K * rank + K)
        for h in range(2):
            def go(h=h):
                trs = []
                for c in far + near:
                    rid, pid = topo.addr(c)[:2]
                    use = lanes[c][h::2] if t == 0 and OPT["halves"] else lanes[c]
                    trs.append(RemoteDMATransfer(dst_ids=[DstId(rid=rid, pnc=pid)], dma_engine_mask=sum(1 << e for e in use),
                                                 remote_sem=T.sem["arr%d" % t], src=raw(src[h]), dst=raw(dst[h])))
                return g.remote_dma_fused(trs, local_sem=T.sem.snd)
            op("g", go, r=[src[h]])
            if t == 0:
                dma("y", lambda h=h: raw(dst[h]), lambda h=h: raw(src[h]), r=[src[h]], sem=T.sem["arr%d" % t])
        land = [a for c in range(N) if t == 0 or c != rank for a in pair("m%d" % t, K * c, K * c + K)]
        op(None, None, w=land, sem=(T.sem["arr%d" % t], counts[t] + 32 * (1 - t)))

    zer = lambda n, p0=0, p1=128: reg("zer", 0, n, 1, p0, p1)
    bank = lambda name, b, n, p0=0, p1=128: reg(name, 512 * b, 512 * b + n, 1, p0, p1)
    E = lambda b, n=128: pair("m0", NK + 128 * b, NK + 128 * b + n)
    base = [128, 0, 0]
    X = lambda t, c0, c1: pair("x%d" % t, base[t] + c0, base[t] + c1)

    dma("y", lambda: T.ut[:], lambda: T.u[:], w=[reg("ut", 0, 4)])
    dma("y", lambda: T.xt[:], lambda: T.x[:], w=[reg("xt", 0, 4 * P)])

    def et():
        fill(reg("et", 0, 524), 0.0)

    def zeros():
        fill(zer(512), 0.0)
        for a in [reg("ct", 4 * P, 1024), reg("gt", 512, 4 * P)] + [reg("mt", 512 * b, 512 * b + 512) for b in range(4)] + [reg("rt", 4 * P, 1024)]:
            dma("y", lambda a=a: ap(a), lambda a=a: ap(zer(a[2] - a[1])), r=[zer(512)], w=[a])

    def ub():
        for b in range(3):
            ts(reg("ub", b, 512, 4), zer(128), reg("ut", b, b + 1), A.add)

    def ktg():
        fill(reg("kt", 0, 512, 4), GAP)
        fill(reg("kt", 2, 512, 4, 64, 128), GAP)
    play({"sel": lambda: sel(reg("et", 7, 519, 4), reg("et", 7, 519, 4), A.not_equal, 1.0),
          "dig": lambda: iota(reg("dig", 0, P, 1, 0, 64), [[0, P // 16], [1, 16]]),
          "hi": lambda: iota(reg("ct", 3, 4 * P, 4, 0, 1), [[16, P // 16], [0, 16]]),
          "gt2": lambda: act(reg("gt", 2, 512, 4), zer(128), F.Copy),
          "one": lambda: act(reg("ct", 1, 4 * P, 2), zer(2 * P), F.Identity, 1.0),
          "kt2": lambda: act(reg("kt", 2, 512, 4, 0, 64), zer(128, 0, 64), F.Copy),
          "ub3": lambda: act(reg("ub", 3, 512, 4), zer(128), F.Identity, reg("ut", 3, 4)),
          "ka": lambda: act(reg("kt", 1, 512, 4, 32, 33), reg("dig", 0, 128, 1, 32, 33), F.Copy, scale=-GAP),
          "kb": lambda: act(reg("kt", 259, 512, 4, 32, 33), zer(64, 32, 33), F.Identity, -16 * GAP),
          "kc": lambda: act(reg("kt", 1, 512, 2, 0, 1), zer(256, 0, 1), F.Identity, 1.0),
          "lo": lambda: act(reg("ct", 1, 4 * P, 4, 0, 1), reg("dig", 0, P, 1, 0, 1), F.Copy),
          "et": et, "zer": zeros, "gtf": lambda: fill(reg("gt", 1, 512, 2), 0.0), "ktf": lambda: fill(reg("kt", 1, 512, 2), 0.0),
          "scan": lambda: scan(reg("gt", 0, 512, 4), zer(128), reg("et", 3, 515, 4), 0.0, A.add),
          "qe": lambda: quant("m0", NK, 128, "et", 7), "ub": ub, "qtri": lambda: quant("x0", base[0] + P, 128, "gt"),
          "qu": lambda: quant("u", 0, 128, "ub"), "qx": lambda: quant("x0", base[0], P, "xt"), "ktg": ktg,
          "qk": lambda: quant("k0", 0, 128, "kt")}, OPT["pre"])

    naA, naB = reg("na", 0, 1), reg("na", 1, 2)
    parts = {"0": (0, 0, P, 0), "1": (1, 0, P, 0), "2": (2, 0, P, 0), "3a": (3, 0, 128, 0), "3b": (3, 64, P, 128)}
    home = {name: ("pr", 0) if name == "0" else ("px", 512 * OPT["bank"][name]) for name in parts}
    wide = lambda name: reg(home[name][0], home[name][1], home[name][1] + parts[name][2] - parts[name][1])
    used = lambda name: reg(home[name][0], home[name][1] + parts[name][3] - parts[name][1], home[name][1] + parts[name][2] - parts[name][1])
    held = lambda name: reg("dx", P * (parts[name][0] - 1) + parts[name][3], P * (parts[name][0] - 1) + parts[name][2])
    kept = OPT["kept"].split()
    into = [bank("pr", 0, P)]
    for t in range(R):
        kk, m = "k%d" % t, "m%d" % t
        tri = (lambda c0, c1: reg("px", 1536 + 2 + c0, 1536 + 2 + c1)) if t == 0 else (lambda c0, c1: reg("pr", P + c0, P + c1))
        d = {}

        def aside():
            for name in kept:
                mm(wide(name), E(parts[name][0]), X(t, parts[name][1], parts[name][2]))
            for name in kept:
                act(held(name), used(name), F.Copy)

        steps = {
            "mR": lambda: mm(bank("pu", 0, P), pair("u", 0, 128), X(t, 0, P)),
            "mA": lambda: mm(bank("pu", 1, 128), X(t, 0, 128), pair("u", 0, 128)),
            "mB": lambda: mm(bank("pu", 2, 128), X(t, 64, P), pair("u", 0, 128)),
            "aL": lambda: act(reg("ar", 0, 64), bank("pu", 0, 64), F.Abs),
            "aH": lambda: act(reg("ar", 64, P), reg("pu", 64, P), F.Abs),
            "rA": lambda: red(naA, bank("pu", 1, 1), A.max, True, True),
            "rB": lambda: red(naB, bank("pu", 2, 1), A.max, True, True),
            "s0": lambda: act(reg("dd", 0, 64), reg("ar", 0, 64), F.Sign, naA),
            "s1": lambda: act(reg("dd", 64, 128), reg("ar", 64, 128), F.Sign, naA),
            "s2": lambda: act(reg("dd", 128, P), reg("ar", 128, P), F.Sign, naB),
            "tA": lambda: ts(reg("ct", 512, 4 * P, 4), reg("ar", 128, P), naA, A.add, 0.0, A.is_le),
            "tB": lambda: ts(reg("ct", 2, 512, 4), reg("ar", 0, 128), naB, A.add, 0.0, A.is_lt),
            "t0": lambda: tt(reg("ct", 0, 256, 4), reg("dd", 0, 64), tri(0, 64), A.is_lt),
            "t1": lambda: tt(reg("ct", 256, 512, 4), reg("dd", 64, 128), tri(64, 128), A.is_lt),
            "t2": lambda: tt(reg("ct", 514, 4 * P, 4), reg("dd", 128, P), tri(64, 128), A.is_lt),
            "q0": lambda: quant("c", 0, 128, "ct", 0),
            "q1": lambda: quant("c", 128, 128, "ct", 512),
        }
        if t == 0:
            steps["mT"] = lambda: mm(bank("px", 3, 130), E(0), X(0, P - 2, P + 128))
        else:
            steps["qk"] = lambda: quant(kk, 0, 128, "kt")
        play(steps, OPT["ch%d" % t])
        if t == 1:
            aside()
            quant("w", 0, 128, "wt")
        else:
            act(reg("mt", 128, 512, 4, 0, NK), reg("et", 7, 7 + 4 * NK, 4, 0, NK), F.Identity, -BIG, BIG)
            quant("x0", 0, 128, "mt")
            act(reg("two", 0, NPOW), zer(NPOW), F.Identity, 2.0)
            act(reg("gt", 0, 512, 4, NK, 128), zer(128, NK, 128), F.Copy)
            act(reg("kt", 1, 512, 4, 64, 65), zer(128, 64, 65), F.Identity, 1.0)
        for h in range(2):
            mm(bank("pu", 1 - h, 128), pair(kk, 0, 128), pair("c", 128 * h, 128 * h + 128))
        for h in range(2):
            red(reg("pla", h, h + 1), bank("pu", 1 - h, 128 - 64 * h), A.min, False, True)
        gap = 2 if OPT["two"] else 1
        for c in range(2):
            for half in range(2):
                ts(reg("off%d" % t, gap * c, gap * c + 1, 1, 64 * half, 64 * half + 64), reg("pla", 0, 1, 1, 64 * c, 64 * c + 64),
                   reg("pla", 1, 2, 1, 64 * c, 64 * c + 64), A.min)
        if OPT["two"]:
            for c in range(2):
                pick("l%d" % t, LAY * t + 16 * c, 16, "x%d" % t, base[t], reg("off%d" % t, 2 * c, 2 * c + 1))
        else:
            pick("l%d" % t, LAY * t, 32, "x%d" % t, base[t], reg("off%d" % t, 0, 2))
        send(t)
        ts(reg("plf", t, t + 1), reg("pla", 0, 1), reg("pla", 1, 2), A.min)

        if t == 0:
            for b in (2, 3, 1):
                quant("m0", NK + 128 * b, 128, "et", 7 - b)
            scan(reg("up", 0, NPOW), reg("two", 0, NPOW), zer(NPOW), 2.0 ** -64)
            for h in range(2):
                act(reg("ct", 512 * h + 1, 512 + 256 * h, 4, 64, 65), bank("pu", 1 - h, 128 - 64 * h, 64, 65), F.Relu,
                    2048.0 * ((K - 16) * GAP - 256.0), -2048.0)
            d["0"] = mm(bank("pr", 0, P + 128), E(0), X(0, 0, P + 128), True, False)
        else:
            quant("l1", NK, 128, "zer")
            d["0"] = mm(into[0], E(0), X(t, 0, P), True, False)
        mask = mm(bank("px", 0, 128), E(0), pair("x0", base[0] - NK, base[0] - NK + 128), True, False)
        if t == 0:
            quant("l1", 0, 128, "zer")
            aside()
            mm(bank("pu", 0, 128), pair("c", 0, 128), pair(kk, 0, 128))
            mm(bank("pu", 2, 128), pair("c", 64, P), pair(kk, 0, 128))
            act(reg("fr", 0, 1), bank("pu", 0, 1), F.Sign, 256.0 - K * GAP)
            act(reg("fr", 1, 2), bank("pu", 2, 1), F.Sign, 256.0 - K * GAP)
        else:
            mm(bank("pu", 1, 128), pair("w", 0, 128), pair("m0", 0, 128))
            act(reg("ys", 0, NK), bank("pu", 1, NK), F.Copy)

        def weights():
            for c in range(2):
                act(reg("kt", 2 * c, 512, 4), reg("kt", 2 * c, 512, 4), F.Relu, scale=reg("fr", c, c + 1))

        M = pair(m, 0, 128)
        ne = OPT["ne"]
        outb = [bank("px", 0, 128), bank("px", 3, P), bank("px", 1, 128 * ne), bank("px", 2, 512 - 128 * ne)]
        side = lambda a: [a, X(t, 0, P), E(0, 128 * ne), E(ne, 512 - 128 * ne)]
        early, ya = [[mask], [], [], []], []
        if t == 1:
            mine = pair("l1", LAY - K * rank, LAY - K * rank + 128)
            for i in range(4):
                early[i].append(mm(outb[i], mine, side(mine)[i], i > 0, False, early[i]))
            ya.append(mm(bank("pu", 2, 128), pair("w", 0, 128), mine, True, False))
        with_m = lambda i: mm(outb[i], M, side(M)[i], not early[i], True, early[i])

        def first():
            got = with_m(0)
            if t == 0:
                for a, b in zip(pair("m1", K * rank, K * rank + K) + pair("m1", NK, 128), pair("l1", 0, K) + pair("l1", 0, 32)):
                    dma("y", lambda a=a: raw(a), lambda b=b: raw(b), r=[b], w=[a], after=[got])
                dma("y", lambda: T.wt[:], lambda: T.w[:], w=[reg("wt", 0, 512)], after=[got])
            else:
                store("y", lambda: T.y[:, 0:NK], reg("ys", 0, NK), [got])
            for c, n in ((0, 16), (1, K - 16)):
                store("y", lambda t=t, c=c, n=n: T.pl[0:1, K * t + 16 * c:K * t + 16 * c + n], reg("plf", t, t + 1, 1, 64 * c, 64 * c + n), [got])

        def again(name):
            if name not in kept:
                d[name] = mm(wide(name), E(parts[name][0]), X(t, parts[name][1], parts[name][2]), True, False)

        def fix(name):
            b, acc = parts[name][0], [d[name]] if name in d else []
            mm(wide(name), pair("mt", 128 * b, 128 * b + 128), pair("g", parts[name][1], parts[name][2]), not acc, True, acc)

        def done(name):
            b, c0, c1 = parts[name][0], parts[name][3], parts[name][2]
            if name in kept:
                tt(reg("rt", 4 * c0 + b, 4 * c1, 4), used(name), held(name), A.add)
            else:
                act(reg("rt", 4 * c0 + b, 4 * c1, 4), used(name), F.Copy)

        def out_y():
            act(reg("ys", NK, 2 * NK), bank("pu", 2, NK), F.Copy)
            store("y", lambda: T.y[:, NK:2 * NK], reg("ys", NK, 2 * NK))

        def table(c0, n):
            quant("x%d" % (t + 1), c0, n, "rt", 4 * c0)
            if t + 1 == R:
                c1 = min(c0 + n, P)
                store("y", lambda: T.oc[:, 4 * c0:4 * c1], reg("x%dq" % R, c0, c1))
        at = lambda b: 512 + 128 * b if b < ne else 1024 + 128 * (b - ne)
        turned = lambda b: act(reg("mt", 512 * b, 512 * b + 512, 4, 0, NK), reg("px", at(b), at(b) + 128, 1, 0, NK), F.Copy)
        rows = lambda name, c0, c1, step=1: reg(name, c0, c1, step, 0, NK)
        none = lambda: None
        play({
            "mM": first, "mG": lambda: with_m(1), "mE0": lambda: with_m(2), "mE1": lambda: with_m(3),
            "red": lambda: red(rows("dv", 0, 1), rows("px", 0, NK), A.max),
            "gb": lambda: act(rows("gb", 0, P), rows("px", 1536, 1536 + P), F.Copy),
            "c0": lambda: turned(0), "c1": lambda: turned(1), "c2": lambda: turned(2), "c3": lambda: turned(3),
            "fac": lambda: ts(rows("fac", 0, NPOW), rows("up", 0, NPOW), rows("dv", 0, 1), A.is_gt, 0.5, A.max),
            "scan": lambda: scan(rows("hs", 0, NPOW), rows("fac", 0, NPOW), zer(NPOW, 0, NK), -0.25 * 2.0 ** 64),
            "C": lambda: ts(rows("gt", 0, 4 * P, 4), rows("gb", 0, P), rows("hs", NPOW - 1, NPOW), A.mult),
            "qg": lambda: quant("g", 0, P, "gt"),
            "q0": lambda: quant("mt", 0, 128, "mt", 0), "q1": lambda: quant("mt", 128, 128, "mt", 512),
            "q2": lambda: quant("mt", 256, 128, "mt", 1024), "q3": lambda: quant("mt", 384, 128, "mt", 1536),
            "my": (lambda: mm(bank("pu", 2, 128), pair("w", 0, 128), M, False, True, ya)) if t == 1 else none,
            "cy": out_y if t == 1 else weights,
            **{"k" + name: (lambda name=name: fix(name)) for name in parts}, **{"o" + name: (lambda name=name: done(name)) for name in parts},
            **{"j" + name: (lambda name=name: again(name)) for name in parts if name != "0"},
            "qA": lambda: table(0, 128) if OPT["split"][t] else None, "qB": lambda: table(128, 128) if OPT["split"][t] else table(0, P),
        }, OPT["df%d" % t])

    for k in range(4):
        store("s" if k < 3 else "y", lambda k=k: T.osc[4 * k:4 * k + 4, :], reg("x%ds" % R, 0, P, 1, 32 * k, 32 * k + 4))
    emit(ops, queues, T)
    Y.wait_ge(T.sem.out, 16 * len(outs))
    g.wait_ge(T.sem.snd, sum(counts))
